import numpy as np
import ml_dtypes


def mxq(x, axis, fmt="e4m3"):
    dtype, down = {"e4m3": (ml_dtypes.float8_e4m3fn, 7), "e5m2": (ml_dtypes.float8_e5m2, 14)}[fmt]
    v = np.moveaxis(np.asarray(x, np.float32).astype(ml_dtypes.bfloat16).astype(np.float64), axis, -1)
    blocks = v.reshape(v.shape[:-1] + (-1, 32))
    amax = np.abs(blocks).max(-1, keepdims=True)
    byte = np.maximum(np.where(amax > 0, np.frexp(amax)[1] - 1 + 127, 0) - down, 1)
    scale = np.exp2(byte - 127.0)
    codes = (blocks / scale).astype(np.float32).astype(dtype).astype(np.float64)
    return np.moveaxis((codes * scale).reshape(v.shape), -1, axis)


WIDE = False


def mx_kscale(k):
    if not WIDE:
        return np.ones(k)
    levels = np.array([10, -10, 5, -5, 0])
    if k % 512:
        return np.exp2(np.random.permutation(np.resize(levels, k // 32))).repeat(32)
    a = np.empty((k // 512, 16))
    for p in range(k // 512):
        a[p, :8] = np.random.permutation(np.resize(levels, 8))
        for g in range(8):
            far = levels[np.abs(levels - a[p, g]) >= 10]
            a[p, g + 8] = far[np.random.randint(len(far))]
    return np.exp2(a.ravel()).repeat(32)


def f64(x):
    return np.asarray(x).astype(np.float64)


def striped(idx):
    return np.tile(idx.reshape(-1, 16).T, (8, 1)).astype(np.uint16)


def unstriped(offs):
    return offs[:16].T.reshape(-1).astype(np.int64)


def pack_weight(w):
    k, n = w.shape
    w = f64(np.asarray(w, np.float32).astype(ml_dtypes.bfloat16)).reshape(k // 32, 32, n)
    amax = np.abs(w).max(1)
    byte = np.clip(np.where(amax > 0, np.frexp(amax)[1] - 1 + 127 - 7, 1), 1, 254)
    scaled = (w * np.exp2(127.0 - byte)[:, None, :]).reshape(k, n).astype(np.float32)
    words = np.ascontiguousarray(scaled.reshape(k // 512, 128, 4, n).transpose(0, 1, 3, 2)).astype(ml_dtypes.float8_e4m3fn).view(np.uint8)
    return words, np.ascontiguousarray(byte.astype(np.uint8).reshape(k // 512, 16, n))


def unpack_weight(words, scales):
    g, p, n, _ = words.shape
    vals = np.ascontiguousarray(words).view(ml_dtypes.float8_e4m3fn).astype(np.float64) * np.repeat(np.exp2(scales.astype(np.float64) - 127.0), 8, axis=1)[..., None]
    return vals.transpose(0, 1, 3, 2).reshape(g * 512, n)


def relu(v):
    return np.maximum(v, 0.0)


K, T, S, D, V, H, N = 512, 1024, 512, 3, 256, 512, 128
P = 2 ** 7


def setup_inputs():
    n = np.random.standard_normal
    s = mx_kscale(K)[:, None]
    u = mx_kscale(H)
    near = np.random.permutation(S)
    packed_xT = pack_weight(n((K, T)) * s)
    packed_w2 = pack_weight(n((H, N)) / np.sqrt(3 * H) / u[:, None])
    packed_w3 = pack_weight(n((H, N)) / np.sqrt(3 * H) / u[:, None])
    packed_w4 = pack_weight(n((H, N)) / np.sqrt(3 * H) / u[:, None])
    return {
        "x_words": packed_xT[0],
        "x_scales": packed_xT[1],
        "w1": (n((K, H)) / np.sqrt(K) / s * u).astype(np.float32),
        "w2_words": packed_w2[0],
        "w2_scales": packed_w2[1],
        "w3_words": packed_w3[0],
        "w3_scales": packed_w3[1],
        "w4_words": packed_w4[0],
        "w4_scales": packed_w4[1],
        "gate": (np.tile(np.random.uniform(0.2, 1.0, (D, 1, V)) / np.sqrt(D), (1, P, 1))).astype(np.float32),
        "gate2": (np.tile(np.random.uniform(0.2, 1.0, (D, 1, V)) / np.sqrt(D), (1, P, 1))).astype(np.float32),
        "offs": striped(np.random.permutation(T)[:S]),
        "cen": striped(np.random.permutation(S)[:V]),
        "pos1": striped(near[:V]),
        "pos2": striped(near[V:]),
        "pos3": striped(np.random.permutation(S)[:V]),
        "far1": striped(np.random.permutation(S)[:V]),
        "far2": striped(np.random.permutation(S)[:V]),
        "far3": striped(np.random.permutation(S)[:V]),
    }


def reference(x_words, x_scales, w1, w2_words, w2_scales, w3_words, w3_scales, w4_words, w4_scales, gate, gate2, offs, cen, pos1, pos2, pos3, far1, far2, far3):
    xq = unpack_weight(x_words, x_scales)[:, unstriped(offs)]
    h = relu(mxq(f64(w1), 0, "e4m3").T @ xq)
    z0 = h[:, unstriped(cen)]
    z1 = h[:, unstriped(pos1)] * f64(gate)[0, :1] + h[:, unstriped(pos2)] * f64(gate)[1, :1] + h[:, unstriped(pos3)] * f64(gate)[2, :1]
    z2 = h[:, unstriped(far1)] * f64(gate2)[0, :1] + h[:, unstriped(far2)] * f64(gate2)[1, :1] + h[:, unstriped(far3)] * f64(gate2)[2, :1]
    return np.tanh(unpack_weight(w2_words, w2_scales).T @ mxq(z0, 0, "e4m3") + unpack_weight(w3_words, w3_scales).T @ mxq(z1, 0, "e4m3") + unpack_weight(w4_words, w4_scales).T @ mxq(z2, 0, "e4m3"))

@@ -1,0 +1,170 @@
+from contextlib import ExitStack
+
+import concourse.mybir as mybir
+from concourse.masks import make_identity
+
+K, T, S, D, V, H, N = 512, 1024, 512, 3, 256, 512, 128
+FLOPS = 2 * K * H * S + 3 * 2 * H * N * V
+
+F32 = mybir.dt.float32
+BF16 = mybir.dt.bfloat16
+I32 = mybir.dt.int32
+U32 = mybir.dt.uint32
+U16 = mybir.dt.uint16
+U8 = mybir.dt.uint8
+FP8X4 = mybir.dt.float8_e4m3fn_x4
+ACT = mybir.ActivationFunctionType
+
+P = 128
+PACK = 4
+HALVES = V // P
+
+
+def tile_picked_zmix_tanh_p_kernel(
+    tc, x_words, x_scales, w1, w2_words, w2_scales, w3_words, w3_scales, w4_words, w4_scales,
+    gate, gate2, offs, cen, pos1, pos2, pos3, far1, far2, far3, out,
+):
+    nc = tc.nc
+    with ExitStack() as ctx:
+        keep = ctx.enter_context(tc.tile_pool(name="keep", bufs=1))
+        pairs = ctx.enter_context(tc.tile_pool(name="pairs", bufs=2))
+        banks = ctx.enter_context(tc.psum_pool(name="banks", bufs=1))
+        turned = ctx.enter_context(tc.psum_pool(name="turned", bufs=4))
+
+        def load_list(src, name):
+            held = keep.tile(list(src.shape), U16, name=name)
+            nc.sync.dma_start(held[:], src)
+            return held
+
+        def load_scale_rows(queue, plane, scales):
+            for q in range(4):
+                queue.dma_start(plane[32 * q : 32 * q + 4, :].bitcast(I32), scales[0, 4 * q : 4 * q + 4, :].bitcast(I32))
+
+        def load_words(words, name):
+            held = keep.tile([P, words.shape[2]], I32, name=name, align_bytes=64)
+            nc.sync.dma_start(held[:], words[0].rearrange("p n r -> p (n r)").bitcast(I32))
+            return held
+
+        x_plane = keep.tile([P, T], U8, name="x_plane", align_bytes=64)
+        nc.gpsimd.memset(x_plane[:].bitcast(I32), 0)
+        load_scale_rows(nc.sync, x_plane, x_scales)
+        warm_in = keep.tile([P, 1], F32, name="warm_in")
+        warm_out = keep.tile([P, 1], F32, name="warm_out")
+        nc.vector.memset(warm_in[:], 0.0)
+        nc.scalar.activation(warm_out[:], warm_in[:], ACT.Tanh)
+
+        offs_t = load_list(offs, "offs_t")
+        w1_rows = w1.rearrange("(p j) c -> p j c", j=PACK)
+        w1_a = keep.tile([P, PACK, H // 2], F32, name="w1_a")
+        w1_b = keep.tile([P, PACK, H // 2], F32, name="w1_b")
+        nc.sync.dma_start(w1_a[:], w1_rows[:, :, : H // 2])
+        x_table = load_words(x_words, "x_table")
+        nc.sync.dma_start(w1_b[:], w1_rows[:, :, H // 2 :])
+
+        gate_cols = []
+        hops = []
+        for z, (weights, srcs) in enumerate(((gate, (pos1, pos2, pos3)), (gate2, (far1, far2, far3)))):
+            hops.append([load_list(src, "hop%d_%d" % (z, d)) for d, src in enumerate(srcs)])
+            cols = keep.tile([P, D * HALVES], F32, name="gate_cols%d" % z)
+            half_rows = weights.rearrange("d r (u p) -> (d r u) p", p=P)
+            with nc.allow_non_contiguous_dma(reason="one gate value a partition"):
+                nc.sync.dma_start(cols[:], half_rows[:: P + 1, :].rearrange("i p -> p i"))
+            gate_cols.append(cols)
+        cen_t = load_list(cen, "cen_t")
+
+        ident = keep.tile([P, P], F32, name="ident")
+        make_identity(nc, ident[:])
+
+        w_words = [load_words(words, "w_words%d" % i) for i, words in enumerate((w2_words, w3_words, w4_words))]
+        w_planes = []
+        for i, scales in enumerate((w2_scales, w3_scales, w4_scales)):
+            plane = keep.tile([P, N], U8, name="w_plane%d" % i, align_bytes=64)
+            nc.gpsimd.memset(plane[:].bitcast(I32), 0)
+            load_scale_rows(nc.sync, plane, scales)
+            w_planes.append(plane)
+
+        x_scale = keep.tile([P, S], U8, name="x_scale", align_bytes=64)
+        x_codes = keep.tile([P, S], U32, name="x_codes", align_bytes=64)
+        nc.vector.tensor_copy(x_scale[:], x_plane[:].indirect(offs_t[:]))
+        nc.vector.tensor_copy(x_codes[:], x_table[:].bitcast(U32).indirect(offs_t[:]))
+
+        w1_bf = keep.tile([P, PACK, P, PACK], BF16, name="w1_bf", align_bytes=64)
+
+        def deal(copy, raw, first, m0, m1):
+            copy(
+                w1_bf[:, :, m0:m1, :].rearrange("p t m j -> p m t j"),
+                raw[:, :, PACK * (m0 - first) : PACK * (m1 - first)].rearrange("p j (m t) -> p m t j", t=PACK),
+            )
+
+        deal(nc.scalar.copy, w1_a, 0, 0, 64)
+        deal(nc.scalar.copy, w1_b, 64, 64, 88)
+        deal(nc.vector.tensor_copy, w1_b, 64, 88, 128)
+
+        w1_codes = keep.tile([P, PACK, P], U32, name="w1_codes", align_bytes=64)
+        w1_plane = keep.tile([P, PACK, P], U8, name="w1_plane", align_bytes=64)
+        h = []
+        for t, tag in enumerate(("sum00", "sum01", "sum10", "sum11")):
+            nc.vector.quantize_mx(
+                out=w1_codes[:, t, :].bitcast(FP8X4), scales=w1_plane[:, t, :],
+                in_=w1_bf[:, t, :, :].rearrange("p m j -> p (m j)"),
+            )
+            acc = banks.tile([P, S], F32, name="h_acc%d" % t, tag=tag)
+            nc.tensor.matmul_mx(
+                out=acc[:], lhsT=w1_codes[:, t, :].bitcast(FP8X4), lhsT_scale=w1_plane[:, t, :],
+                rhs=x_codes[:].bitcast(FP8X4), rhs_scale=x_scale[:], start=True, stop=True,
+            )
+            h_t = keep.tile([P, S], F32, name="h%d" % t)
+            nc.scalar.activation(h_t[:], acc[:], ACT.Relu)
+            h.append(h_t)
+
+        def quantize(values, name):
+            codes = keep.tile([P, V], U32, name=name + "_codes", align_bytes=64)
+            plane = keep.tile([P, V], U8, name=name + "_plane", align_bytes=64)
+            nc.vector.quantize_mx(out=codes[:].bitcast(FP8X4), scales=plane[:], in_=values[:].rearrange("p v t -> p (v t)"))
+            return codes, plane
+
+        z_bf = []
+        for z in range(2):
+            sums = [banks.tile([P, PACK, P], F32, name="sum%d%d" % (z, u), tag="sum%d%d" % (z, u)) for u in range(HALVES)]
+            for d in range(D):
+                across = [turned.tile([P, PACK, P], F32, name="across%d" % u, tag="across") for u in range(HALVES)]
+                picked = pairs.tile([P, PACK, V], F32, name="picked")
+                for t in range(PACK):
+                    nc.vector.tensor_copy(picked[:, t, :], h[t][:].indirect(hops[z][d][:]))
+                    for u in range(HALVES):
+                        nc.tensor.transpose(across[u][:, t, :], picked[:, t, u * P : (u + 1) * P], ident[:])
+                for u in range(HALVES):
+                    scaled = keep.tile([P, PACK, P], F32, name="scaled%d%d%d" % (z, d, u))
+                    nc.scalar.activation(scaled[:], across[u][:], ACT.Copy, scale=gate_cols[z][:, HALVES * d + u : HALVES * d + u + 1])
+                    for t in range(PACK):
+                        nc.tensor.matmul(
+                            sums[u][:, t, :], lhsT=scaled[:, t, :], rhs=ident[:], is_transpose=True,
+                            start=(d == 0 and t == 0), stop=(d == D - 1 and t == PACK - 1),
+                        )
+            values = keep.tile([P, V, PACK], BF16, name="z_bf%d" % z, tag="z_bf%d" % z, align_bytes=64)
+            for u in range(HALVES):
+                nc.scalar.copy(values[:, u * P : (u + 1) * P, :], sums[u][:].rearrange("p t v -> p v t"))
+            z_bf.append(values)
+
+        z1_q = quantize(z_bf[0], "z1")
+
+        own = pairs.tile([P, PACK, V], BF16, name="own", tag="picked")
+        for t in range(PACK):
+            nc.vector.tensor_copy(own[:, t, :], h[t][:].indirect(cen_t[:]))
+        z0_bf = keep.tile([P, V, PACK], BF16, name="z0_bf", align_bytes=64)
+        nc.vector.tensor_copy(
+            z0_bf[:].rearrange("p (c i) t -> p c t i", i=4), own[:].rearrange("p t (c i) -> p c t i", i=4)
+        )
+        z0_q = quantize(z0_bf, "z0")
+        z2_q = quantize(z_bf[1], "z2")
+
+        result = banks.tile([P, V], F32, name="result", tag="sum00")
+        passes = ((1, z1_q), (2, z2_q), (0, z0_q))
+        for n, (i, (codes, plane)) in enumerate(passes):
+            nc.tensor.matmul_mx(
+                out=result[:], lhsT=w_words[i][:].bitcast(FP8X4), lhsT_scale=w_planes[i][:],
+                rhs=codes[:].bitcast(FP8X4), rhs_scale=plane[:], start=(n == 0), stop=(n == len(passes) - 1),
+            )
+        staged = keep.tile([P, V], F32, name="staged")
+        nc.scalar.activation(staged[:], result[:], ACT.Tanh)
+        nc.sync.dma_start(out, staged[:])

@@ -47,17 +47,17 @@ def tile_picked_zmix_tanh_p_kernel(
 
         x_plane = keep.tile([P, T], U8, name="x_plane", align_bytes=64)
         nc.gpsimd.memset(x_plane[:].bitcast(I32), 0)
-        load_scale_rows(nc.sync, x_plane, x_scales)
         warm_in = keep.tile([P, 1], F32, name="warm_in")
         warm_out = keep.tile([P, 1], F32, name="warm_out")
         nc.vector.memset(warm_in[:], 0.0)
         nc.scalar.activation(warm_out[:], warm_in[:], ACT.Tanh)
 
-        offs_t = load_list(offs, "offs_t")
         w1_rows = w1.rearrange("(p j) c -> p j c", j=PACK)
         w1_a = keep.tile([P, PACK, H // 2], F32, name="w1_a")
         w1_b = keep.tile([P, PACK, H // 2], F32, name="w1_b")
         nc.sync.dma_start(w1_a[:], w1_rows[:, :, : H // 2])
+        load_scale_rows(nc.sync, x_plane, x_scales)
+        offs_t = load_list(offs, "offs_t")
         x_table = load_words(x_words, "x_table")
         nc.sync.dma_start(w1_b[:], w1_rows[:, :, H // 2 :])
 
@@ -108,19 +108,32 @@ def tile_picked_zmix_tanh_p_kernel(
                 out=w1_codes[:, t, :].bitcast(FP8X4), scales=w1_plane[:, t, :],
                 in_=w1_bf[:, t, :, :].rearrange("p m j -> p (m j)"),
             )
-            acc = banks.tile([P, S], F32, name="h_acc%d" % t, tag=tag)
-            nc.tensor.matmul_mx(
-                out=acc[:], lhsT=w1_codes[:, t, :].bitcast(FP8X4), lhsT_scale=w1_plane[:, t, :],
-                rhs=x_codes[:].bitcast(FP8X4), rhs_scale=x_scale[:], start=True, stop=True,
-            )
             h_t = keep.tile([P, S], F32, name="h%d" % t)
-            nc.scalar.activation(h_t[:], acc[:], ACT.Relu)
+
+            def product(acc, cols):
+                nc.tensor.matmul_mx(
+                    out=acc, lhsT=w1_codes[:, t, :].bitcast(FP8X4), lhsT_scale=w1_plane[:, t, :],
+                    rhs=x_codes[:, cols].bitcast(FP8X4), rhs_scale=x_scale[:, cols], start=True, stop=True,
+                )
+
+            if t == 0:
+                left = banks.tile([P, S // 2], F32, name="h_left", tag=tag)
+                right = turned.tile([P, S // 2], F32, name="h_right", tag="across")
+                product(left[:], slice(0, S // 2))
+                product(right[:], slice(S // 2, S))
+                nc.scalar.activation(h_t[:, : S // 2], left[:], ACT.Relu)
+                nc.vector.tensor_relu(h_t[:, S // 2 :], right[:])
+            else:
+                acc = banks.tile([P, S], F32, name="h_acc%d" % t, tag=tag)
+                product(acc[:], slice(0, S))
+                nc.scalar.activation(h_t[:], acc[:], ACT.Relu)
             h.append(h_t)
 
         def quantize(values, name):
-            codes = keep.tile([P, V], U32, name=name + "_codes", align_bytes=64)
-            plane = keep.tile([P, V], U8, name=name + "_plane", align_bytes=64)
-            nc.vector.quantize_mx(out=codes[:].bitcast(FP8X4), scales=plane[:], in_=values[:].rearrange("p v t -> p (v t)"))
+            width = values.shape[1]
+            codes = keep.tile([P, width], U32, name=name + "_codes", align_bytes=64)
+            plane = keep.tile([P, width], U8, name=name + "_plane", align_bytes=64)
+            nc.vector.quantize_mx(out=codes[:].bitcast(FP8X4), scales=plane[:], in_=values.rearrange("p v t -> p (v t)"))
             return codes, plane
 
         z_bf = []
@@ -146,25 +159,32 @@ def tile_picked_zmix_tanh_p_kernel(
                 nc.scalar.copy(values[:, u * P : (u + 1) * P, :], sums[u][:].rearrange("p t v -> p v t"))
             z_bf.append(values)
 
-        z1_q = quantize(z_bf[0], "z1")
+        z1_q = quantize(z_bf[0][:], "z1")
 
         own = pairs.tile([P, PACK, V], BF16, name="own", tag="picked")
         for t in range(PACK):
             nc.vector.tensor_copy(own[:, t, :], h[t][:].indirect(cen_t[:]))
         z0_bf = keep.tile([P, V, PACK], BF16, name="z0_bf", align_bytes=64)
-        nc.vector.tensor_copy(
-            z0_bf[:].rearrange("p (c i) t -> p c t i", i=4), own[:].rearrange("p t (c i) -> p c t i", i=4)
-        )
-        z0_q = quantize(z0_bf, "z0")
-        z2_q = quantize(z_bf[1], "z2")
-
-        result = banks.tile([P, V], F32, name="result", tag="sum00")
-        passes = ((1, z1_q), (2, z2_q), (0, z0_q))
-        for n, (i, (codes, plane)) in enumerate(passes):
-            nc.tensor.matmul_mx(
-                out=result[:], lhsT=w_words[i][:].bitcast(FP8X4), lhsT_scale=w_planes[i][:],
-                rhs=codes[:].bitcast(FP8X4), rhs_scale=plane[:], start=(n == 0), stop=(n == len(passes) - 1),
+        halves = [slice(u * P, (u + 1) * P) for u in range(HALVES)]
+        for cols in halves:
+            nc.vector.tensor_copy(
+                z0_bf[:, cols, :].rearrange("p (c i) t -> p c t i", i=4), own[:, :, cols].rearrange("p t (c i) -> p c t i", i=4)
             )
-        staged = keep.tile([P, V], F32, name="staged")
-        nc.scalar.activation(staged[:], result[:], ACT.Tanh)
-        nc.sync.dma_start(out, staged[:])
+        z0_q = [quantize(z0_bf[:, cols, :], "z0_%d" % u) for u, cols in enumerate(halves)]
+
+        for u, cols in enumerate(halves):
+            z2_q = quantize(z_bf[1][:, cols, :], "z2_%d" % u)
+            result = banks.tile([P, P], F32, name="result%d" % u, tag="sum1%d" % u)
+            passes = (
+                (1, z1_q[0][:, cols], z1_q[1][:, cols]),
+                (0, z0_q[u][0][:], z0_q[u][1][:]),
+                (2, z2_q[0][:], z2_q[1][:]),
+            )
+            for n, (i, codes, plane) in enumerate(passes):
+                nc.tensor.matmul_mx(
+                    out=result[:], lhsT=w_words[i][:].bitcast(FP8X4), lhsT_scale=w_planes[i][:],
+                    rhs=codes.bitcast(FP8X4), rhs_scale=plane, start=(n == 0), stop=(n == len(passes) - 1),
+                )
+            staged = keep.tile([P, P], F32, name="staged%d" % u)
+            nc.scalar.activation(staged[:], result[:], ACT.Tanh)
+            nc.sync.dma_start(out[:, cols], staged[:])

@@ -18,6 +18,7 @@ ACT = mybir.ActivationFunctionType
 P = 128
 PACK = 4
 HALVES = V // P
+PAIR = 2
 
 
 def tile_picked_zmix_tanh_p_kernel(
@@ -27,9 +28,9 @@ def tile_picked_zmix_tanh_p_kernel(
     nc = tc.nc
     with ExitStack() as ctx:
         keep = ctx.enter_context(tc.tile_pool(name="keep", bufs=1))
-        pairs = ctx.enter_context(tc.tile_pool(name="pairs", bufs=2))
+        pairs = ctx.enter_context(tc.tile_pool(name="pairs", bufs=4))
         banks = ctx.enter_context(tc.psum_pool(name="banks", bufs=1))
-        turned = ctx.enter_context(tc.psum_pool(name="turned", bufs=4))
+        turned = ctx.enter_context(tc.psum_pool(name="turned", bufs=2))
 
         def load_list(src, name):
             held = keep.tile(list(src.shape), U16, name=name)
@@ -118,7 +119,7 @@ def tile_picked_zmix_tanh_p_kernel(
 
             if t == 0:
                 left = banks.tile([P, S // 2], F32, name="h_left", tag=tag)
-                right = turned.tile([P, S // 2], F32, name="h_right", tag="across")
+                right = banks.tile([P, S // 2], F32, name="h_right")
                 product(left[:], slice(0, S // 2))
                 product(right[:], slice(S // 2, S))
                 nc.scalar.activation(h_t[:, : S // 2], left[:], ACT.Relu)
@@ -129,9 +130,9 @@ def tile_picked_zmix_tanh_p_kernel(
                 nc.scalar.activation(h_t[:], acc[:], ACT.Relu)
             h.append(h_t)
 
-        def quantize(values, name):
+        def quantize(values, name, pool=keep, tag=None):
             width = values.shape[1]
-            codes = keep.tile([P, width], U32, name=name + "_codes", align_bytes=64)
+            codes = pool.tile([P, width], U32, name=name + "_codes", tag=tag or name + "_codes", align_bytes=64)
             plane = keep.tile([P, width], U8, name=name + "_plane", align_bytes=64)
             nc.vector.quantize_mx(out=codes[:].bitcast(FP8X4), scales=plane[:], in_=values.rearrange("p v t -> p (v t)"))
             return codes, plane
@@ -140,28 +141,32 @@ def tile_picked_zmix_tanh_p_kernel(
         for z in range(2):
             sums = [banks.tile([P, PACK, P], F32, name="sum%d%d" % (z, u), tag="sum%d%d" % (z, u)) for u in range(HALVES)]
             for d in range(D):
-                across = [turned.tile([P, PACK, P], F32, name="across%d" % u, tag="across") for u in range(HALVES)]
-                picked = pairs.tile([P, PACK, V], F32, name="picked")
-                for t in range(PACK):
-                    nc.vector.tensor_copy(picked[:, t, :], h[t][:].indirect(hops[z][d][:]))
+                for t0 in range(0, PACK, PAIR):
+                    picked = pairs.tile([P, PAIR, V], F32, name="picked", align_bytes=64)
+                    across = turned.tile([P, HALVES, PAIR, P], F32, name="across")
+                    for i in range(PAIR):
+                        nc.vector.tensor_copy(picked[:, i, :], h[t0 + i][:].indirect(hops[z][d][:]))
+                        for u in range(HALVES):
+                            nc.tensor.transpose(across[:, u, i, :], picked[:, i, u * P : (u + 1) * P], ident[:])
                     for u in range(HALVES):
-                        nc.tensor.transpose(across[u][:, t, :], picked[:, t, u * P : (u + 1) * P], ident[:])
-                for u in range(HALVES):
-                    scaled = keep.tile([P, PACK, P], F32, name="scaled%d%d%d" % (z, d, u))
-                    nc.scalar.activation(scaled[:], across[u][:], ACT.Copy, scale=gate_cols[z][:, HALVES * d + u : HALVES * d + u + 1])
-                    for t in range(PACK):
-                        nc.tensor.matmul(
-                            sums[u][:, t, :], lhsT=scaled[:, t, :], rhs=ident[:], is_transpose=True,
-                            start=(d == 0 and t == 0), stop=(d == D - 1 and t == PACK - 1),
+                        scaled = keep.tile([P, PAIR, P], F32, name="scaled%d%d%d%d" % (z, d, t0, u))
+                        nc.scalar.activation(
+                            scaled[:], across[:, u, :, :], ACT.Copy,
+                            scale=gate_cols[z][:, HALVES * d + u : HALVES * d + u + 1],
                         )
+                        for i in range(PAIR):
+                            nc.tensor.matmul(
+                                sums[u][:, t0 + i, :], lhsT=scaled[:, i, :], rhs=ident[:], is_transpose=True,
+                                start=(d == 0 and t0 + i == 0), stop=(d == D - 1 and t0 + i == PACK - 1),
+                            )
             values = keep.tile([P, V, PACK], BF16, name="z_bf%d" % z, tag="z_bf%d" % z, align_bytes=64)
             for u in range(HALVES):
                 nc.scalar.copy(values[:, u * P : (u + 1) * P, :], sums[u][:].rearrange("p t v -> p v t"))
             z_bf.append(values)
 
-        z1_q = quantize(z_bf[0][:], "z1")
+        z1_q = quantize(z_bf[0][:], "z1", pairs, "picked")
 
-        own = pairs.tile([P, PACK, V], BF16, name="own", tag="picked")
+        own = pairs.tile([P, PACK, V], BF16, name="own", tag="picked", align_bytes=64)
         for t in range(PACK):
             nc.vector.tensor_copy(own[:, t, :], h[t][:].indirect(cen_t[:]))
         z0_bf = keep.tile([P, V, PACK], BF16, name="z0_bf", align_bytes=64)

@@ -14,11 +14,14 @@ U16 = mybir.dt.uint16
 U8 = mybir.dt.uint8
 FP8X4 = mybir.dt.float8_e4m3fn_x4
 ACT = mybir.ActivationFunctionType
+MULT = mybir.AluOpType.mult
 
 P = 128
 PACK = 4
 HALVES = V // P
 PAIR = 2
+Q = P // 2
+PICKED_BUFS = 4
 
 
 def tile_picked_zmix_tanh_p_kernel(
@@ -28,23 +31,35 @@ def tile_picked_zmix_tanh_p_kernel(
     nc = tc.nc
     with ExitStack() as ctx:
         keep = ctx.enter_context(tc.tile_pool(name="keep", bufs=1))
-        pairs = ctx.enter_context(tc.tile_pool(name="pairs", bufs=4))
+        ring = ctx.enter_context(tc.tile_pool(name="ring", bufs=PICKED_BUFS))
         banks = ctx.enter_context(tc.psum_pool(name="banks", bufs=1))
-        turned = ctx.enter_context(tc.psum_pool(name="turned", bufs=2))
+        sums = ctx.enter_context(tc.psum_pool(name="sums", bufs=3))
 
         def load_list(src, name):
             held = keep.tile(list(src.shape), U16, name=name)
             nc.sync.dma_start(held[:], src)
             return held
 
-        def load_scale_rows(queue, plane, scales):
+        def load_scale_rows(plane, scales):
             for q in range(4):
-                queue.dma_start(plane[32 * q : 32 * q + 4, :].bitcast(I32), scales[0, 4 * q : 4 * q + 4, :].bitcast(I32))
+                nc.sync.dma_start(plane[32 * q : 32 * q + 4, :].bitcast(I32), scales[0, 4 * q : 4 * q + 4, :].bitcast(I32))
 
         def load_words(words, name):
             held = keep.tile([P, words.shape[2]], I32, name=name, align_bytes=64)
             nc.sync.dma_start(held[:], words[0].rearrange("p n r -> p (n r)").bitcast(I32))
             return held
+
+        def load_gates(weights, name):
+            held = keep.tile([P, D, V], F32, name=name)
+            nc.sync.dma_start(held[:], weights.rearrange("d p v -> p d v"))
+            return held
+
+        w1_rows = w1.rearrange("(p j) c -> p j c", j=PACK)
+
+        w1_raw = [keep.tile([P, PACK, H // 2], F32, name="w1_raw%d" % half) for half in range(2)]
+
+        def load_w1(half, rows):
+            nc.sync.dma_start(w1_raw[half][:, rows, :], w1_rows[:, rows, half * H // 2 : (half + 1) * H // 2])
 
         x_plane = keep.tile([P, T], U8, name="x_plane", align_bytes=64)
         nc.gpsimd.memset(x_plane[:].bitcast(I32), 0)
@@ -53,25 +68,21 @@ def tile_picked_zmix_tanh_p_kernel(
         nc.vector.memset(warm_in[:], 0.0)
         nc.scalar.activation(warm_out[:], warm_in[:], ACT.Tanh)
 
-        w1_rows = w1.rearrange("(p j) c -> p j c", j=PACK)
-        w1_a = keep.tile([P, PACK, H // 2], F32, name="w1_a")
-        w1_b = keep.tile([P, PACK, H // 2], F32, name="w1_b")
-        nc.sync.dma_start(w1_a[:], w1_rows[:, :, : H // 2])
-        load_scale_rows(nc.sync, x_plane, x_scales)
+        load_w1(0, slice(0, PAIR))
         offs_t = load_list(offs, "offs_t")
+        load_scale_rows(x_plane, x_scales)
         x_table = load_words(x_words, "x_table")
-        nc.sync.dma_start(w1_b[:], w1_rows[:, :, H // 2 :])
-
-        gate_cols = []
-        hops = []
-        for z, (weights, srcs) in enumerate(((gate, (pos1, pos2, pos3)), (gate2, (far1, far2, far3)))):
-            hops.append([load_list(src, "hop%d_%d" % (z, d)) for d, src in enumerate(srcs)])
-            cols = keep.tile([P, D * HALVES], F32, name="gate_cols%d" % z)
-            half_rows = weights.rearrange("d r (u p) -> (d r u) p", p=P)
-            with nc.allow_non_contiguous_dma(reason="one gate value a partition"):
-                nc.sync.dma_start(cols[:], half_rows[:: P + 1, :].rearrange("i p -> p i"))
-            gate_cols.append(cols)
+        load_w1(0, slice(PAIR, PACK))
         cen_t = load_list(cen, "cen_t")
+        gate_cols = keep.tile([P, D * HALVES], F32, name="gate_cols")
+        half_rows = gate.rearrange("d r (u p) -> (d r u) p", p=P)
+        with nc.allow_non_contiguous_dma(reason="one gate value a partition"):
+            nc.sync.dma_start(gate_cols[:], half_rows[:: P + 1, :].rearrange("i p -> p i"))
+        near = [load_list(src, "near%d" % d) for d, src in enumerate((pos1, pos2, pos3))]
+        load_w1(1, slice(0, PACK))
+        w1_a, w1_b = [raw[:].rearrange("p j (q t) -> p q j t", t=PACK) for raw in w1_raw]
+        far = [load_list(src, "far%d" % d) for d, src in enumerate((far1, far2, far3))]
+        far_gates = load_gates(gate2, "far_gates")
 
         ident = keep.tile([P, P], F32, name="ident")
         make_identity(nc, ident[:])
@@ -81,115 +92,162 @@ def tile_picked_zmix_tanh_p_kernel(
         for i, scales in enumerate((w2_scales, w3_scales, w4_scales)):
             plane = keep.tile([P, N], U8, name="w_plane%d" % i, align_bytes=64)
             nc.gpsimd.memset(plane[:].bitcast(I32), 0)
-            load_scale_rows(nc.sync, plane, scales)
+            load_scale_rows(plane, scales)
             w_planes.append(plane)
 
+        def quantize(values, name, pool=keep, tag=None):
+            width = values.shape[1] // PACK
+            codes = pool.tile([P, width], U32, name=name + "_codes", tag=tag or name + "_codes", align_bytes=64)
+            plane = keep.tile([P, width], U8, name=name + "_plane", align_bytes=64)
+            nc.vector.quantize_mx(out=codes[:].bitcast(FP8X4), scales=plane[:], in_=values)
+            return codes, plane
+
+        first = keep.tile([P, 2, Q, PACK], BF16, name="first", tag="first", align_bytes=64)
+        second = keep.tile([P, 2, Q, PACK], BF16, name="second", tag="second", align_bytes=64)
+        high = keep.tile([P, PAIR, 2, Q, PACK], BF16, name="high", tag="high", align_bytes=64)
+        for rows in (slice(0, PAIR), slice(PAIR, PACK)):
+            nc.scalar.copy(first[:, :, :, rows].rearrange("p s q j -> p q j s"), w1_a[:, :, rows, :PAIR])
+        nc.scalar.copy(high[:, :, 0, :, :].rearrange("p s q j -> p q j s"), w1_a[:, :, :, PAIR:])
+        nc.scalar.copy(second[:].rearrange("p s q j -> p q j s"), w1_b[:, :, :, :PAIR])
+        nc.scalar.copy(high[:, :, 1, :, :].rearrange("p s q j -> p q j s"), w1_b[:, :, :, PAIR:])
+        w1_bf = [low[:].rearrange("p a q j -> p (a q j)") for low in (first, second)]
+
         x_scale = keep.tile([P, S], U8, name="x_scale", align_bytes=64)
-        x_codes = keep.tile([P, S], U32, name="x_codes", align_bytes=64)
         nc.vector.tensor_copy(x_scale[:], x_plane[:].indirect(offs_t[:]))
+        x_codes = keep.tile([P, S], U32, name="x_codes", align_bytes=64)
         nc.vector.tensor_copy(x_codes[:], x_table[:].bitcast(U32).indirect(offs_t[:]))
+        first_q = quantize(w1_bf[0], "w1_0")
 
-        w1_bf = keep.tile([P, PACK, P, PACK], BF16, name="w1_bf", align_bytes=64)
-
-        def deal(copy, raw, first, m0, m1):
-            copy(
-                w1_bf[:, :, m0:m1, :].rearrange("p t m j -> p m t j"),
-                raw[:, :, PACK * (m0 - first) : PACK * (m1 - first)].rearrange("p j (m t) -> p m t j", t=PACK),
-            )
-
-        deal(nc.scalar.copy, w1_a, 0, 0, 64)
-        deal(nc.scalar.copy, w1_b, 64, 64, 88)
-        deal(nc.vector.tensor_copy, w1_b, 64, 88, 128)
-
-        w1_codes = keep.tile([P, PACK, P], U32, name="w1_codes", align_bytes=64)
-        w1_plane = keep.tile([P, PACK, P], U8, name="w1_plane", align_bytes=64)
         h = []
-        for t, tag in enumerate(("sum00", "sum01", "sum10", "sum11")):
-            nc.vector.quantize_mx(
-                out=w1_codes[:, t, :].bitcast(FP8X4), scales=w1_plane[:, t, :],
-                in_=w1_bf[:, t, :, :].rearrange("p m j -> p (m j)"),
-            )
-            h_t = keep.tile([P, S], F32, name="h%d" % t)
+
+        def make_h(codes, plane):
+            n = len(h)
+            h_n = keep.tile([P, S], F32, name="h%d" % n)
 
             def product(acc, cols):
                 nc.tensor.matmul_mx(
-                    out=acc, lhsT=w1_codes[:, t, :].bitcast(FP8X4), lhsT_scale=w1_plane[:, t, :],
+                    out=acc, lhsT=codes[:].bitcast(FP8X4), lhsT_scale=plane[:],
                     rhs=x_codes[:, cols].bitcast(FP8X4), rhs_scale=x_scale[:, cols], start=True, stop=True,
                 )
 
-            if t == 0:
-                left = banks.tile([P, S // 2], F32, name="h_left", tag=tag)
-                right = banks.tile([P, S // 2], F32, name="h_right")
-                product(left[:], slice(0, S // 2))
-                product(right[:], slice(S // 2, S))
-                nc.scalar.activation(h_t[:, : S // 2], left[:], ACT.Relu)
-                nc.vector.tensor_relu(h_t[:, S // 2 :], right[:])
+            if n == 0:
+                for cols, bank in zip((slice(0, 256), slice(256, 384), slice(384, S)), "ade"):
+                    acc = banks.tile([P, cols.stop - cols.start], F32, name="h_part%d" % cols.start, tag=bank)
+                    product(acc[:], cols)
+                    if cols.start == 0:
+                        nc.vector.tensor_relu(h_n[:, cols], acc[:])
+                    else:
+                        nc.scalar.activation(h_n[:, cols], acc[:], ACT.Relu)
+            elif n == 1:
+                for cols, bank in zip((slice(0, 256), slice(256, S)), "be"):
+                    acc = banks.tile([P, S // 2], F32, name="h_half%d" % cols.start, tag=bank)
+                    product(acc[:], cols)
+                    nc.scalar.activation(h_n[:, cols], acc[:], ACT.Relu)
             else:
-                acc = banks.tile([P, S], F32, name="h_acc%d" % t, tag=tag)
+                acc = banks.tile([P, S], F32, name="h_acc%d" % n, tag="abcd"[n])
                 product(acc[:], slice(0, S))
-                nc.scalar.activation(h_t[:], acc[:], ACT.Relu)
-            h.append(h_t)
+                nc.scalar.activation(h_n[:], acc[:], ACT.Relu)
+            h.append(h_n)
 
-        def quantize(values, name, pool=keep, tag=None):
-            width = values.shape[1]
-            codes = pool.tile([P, width], U32, name=name + "_codes", tag=tag or name + "_codes", align_bytes=64)
-            plane = keep.tile([P, width], U8, name=name + "_plane", align_bytes=64)
-            nc.vector.quantize_mx(out=codes[:].bitcast(FP8X4), scales=plane[:], in_=values.rearrange("p v t -> p (v t)"))
-            return codes, plane
-
-        z_bf = []
-        for z in range(2):
-            sums = [banks.tile([P, PACK, P], F32, name="sum%d%d" % (z, u), tag="sum%d%d" % (z, u)) for u in range(HALVES)]
-            for d in range(D):
-                for t0 in range(0, PACK, PAIR):
-                    picked = pairs.tile([P, PAIR, V], F32, name="picked", align_bytes=64)
-                    across = turned.tile([P, HALVES, PAIR, P], F32, name="across")
-                    for i in range(PAIR):
-                        nc.vector.tensor_copy(picked[:, i, :], h[t0 + i][:].indirect(hops[z][d][:]))
-                        for u in range(HALVES):
-                            nc.tensor.transpose(across[:, u, i, :], picked[:, i, u * P : (u + 1) * P], ident[:])
-                    for u in range(HALVES):
-                        scaled = keep.tile([P, PAIR, P], F32, name="scaled%d%d%d%d" % (z, d, t0, u))
-                        nc.scalar.activation(
-                            scaled[:], across[:, u, :, :], ACT.Copy,
-                            scale=gate_cols[z][:, HALVES * d + u : HALVES * d + u + 1],
-                        )
-                        for i in range(PAIR):
-                            nc.tensor.matmul(
-                                sums[u][:, t0 + i, :], lhsT=scaled[:, i, :], rhs=ident[:], is_transpose=True,
-                                start=(d == 0 and t0 + i == 0), stop=(d == D - 1 and t0 + i == PACK - 1),
-                            )
-            values = keep.tile([P, V, PACK], BF16, name="z_bf%d" % z, tag="z_bf%d" % z, align_bytes=64)
+        make_h(*first_q)
+        near_gates = keep.tile([P, D, V], F32, name="near_gates")
+        for d in range(D):
+            spread = sums.tile([P, HALVES, P], F32, name="spread%d" % d, tag="acc")
             for u in range(HALVES):
-                nc.scalar.copy(values[:, u * P : (u + 1) * P, :], sums[u][:].rearrange("p t v -> p v t"))
-            z_bf.append(values)
+                column = gate_cols[:, HALVES * d + u : HALVES * d + u + 1]
+                nc.tensor.transpose(spread[:, u, :], column.to_broadcast([P, P]), ident[:])
+            nc.scalar.copy(near_gates[:, d, :], spread[:].rearrange("p u v -> p (u v)"))
+        make_h(*quantize(w1_bf[1], "w1_1"))
+        codes, plane = quantize(high[:].rearrange("p s a q j -> p (s a q j)"), "w1_high")
+        for s in range(PAIR):
+            make_h(codes[:, s * P : (s + 1) * P], plane[:, s * P : (s + 1) * P])
 
-        z1_q = quantize(z_bf[0][:], "z1", pairs, "picked")
+        def gather_sum(accs, n, lists, gates):
+            i = n % PAIR
+            for d, held in enumerate(lists):
+                picked = ring.tile([P, V], F32, name="picked", align_bytes=64)[:]
+                if gates is None:
+                    nc.vector.tensor_copy(picked, h[n][:].indirect(held[:]))
+                elif len(accs) == HALVES and i == PAIR - 1 and d == D - 1:
+                    for cols in halves:
+                        window = h[n][:].indirect(held[:, cols.start // 16 : cols.stop // 16])
+                        nc.vector.tensor_tensor(picked[:, cols], window, gates[:, d, cols], MULT)
+                else:
+                    nc.vector.tensor_tensor(picked, h[n][:].indirect(held[:]), gates[:, d, :], MULT)
+                per_bank = HALVES // len(accs)
+                for u in range(HALVES):
+                    nc.tensor.matmul(
+                        accs[u // per_bank][:, u % per_bank, i, :], lhsT=picked[:, u * P : (u + 1) * P], rhs=ident[:], is_transpose=True,
+                        start=(d == 0 and i == 0 and u % per_bank == 0),
+                        stop=(d == len(lists) - 1 and i == PAIR - 1 and u % per_bank == per_bank - 1),
+                    )
 
-        own = pairs.tile([P, PACK, V], BF16, name="own", tag="picked", align_bytes=64)
-        for t in range(PACK):
-            nc.vector.tensor_copy(own[:, t, :], h[t][:].indirect(cen_t[:]))
-        z0_bf = keep.tile([P, V, PACK], BF16, name="z0_bf", align_bytes=64)
+        def turn_back(accs, a, backs, name):
+            per_bank = HALVES // len(accs)
+            for b, acc in enumerate(accs):
+                rounded = keep.tile([P, per_bank, P, PAIR], BF16, name="rounded%s%d%d" % (name, a, b))
+                if a == 0:
+                    nc.scalar.copy(
+                        rounded[:].rearrange("v u (i q) s -> v u i q s", i=PAIR), acc[:].rearrange("v u i (s q) -> v u i q s", s=PAIR)
+                    )
+                else:
+                    nc.scalar.copy(rounded[:], acc[:].rearrange("v u s p -> v u p s"))
+                for u in range(per_bank):
+                    words = rounded[:, u, :, :].rearrange("v p s -> v (p s)").bitcast(F32)
+                    nc.tensor.transpose(backs[b * per_bank + u], words, ident[:])
+
+        def sum_tiles(count):
+            return [sums.tile([P, HALVES // count, PAIR, P], F32, name="acc", tag="acc") for b in range(count)]
+
+        def words_of(values):
+            return values.rearrange("p v t -> p (v t)").bitcast(F32).rearrange("p (v a) -> p v a", a=PACK // PAIR)
+
         halves = [slice(u * P, (u + 1) * P) for u in range(HALVES)]
-        for cols in halves:
-            nc.vector.tensor_copy(
-                z0_bf[:, cols, :].rearrange("p (c i) t -> p c t i", i=4), own[:, :, cols].rearrange("p t (c i) -> p c t i", i=4)
-            )
-        z0_q = [quantize(z0_bf[:, cols, :], "z0_%d" % u) for u, cols in enumerate(halves)]
+        z_bf = [keep.tile([P, V, PACK], BF16, name="z_bf%d" % z, align_bytes=64) for z in range(3)]
 
-        for u, cols in enumerate(halves):
-            z2_q = quantize(z_bf[1][:, cols, :], "z2_%d" % u)
-            result = banks.tile([P, P], F32, name="result%d" % u, tag="sum1%d" % u)
-            passes = (
-                (1, z1_q[0][:, cols], z1_q[1][:, cols]),
-                (0, z0_q[u][0][:], z0_q[u][1][:]),
-                (2, z2_q[0][:], z2_q[1][:]),
+        own_acc = sum_tiles(1)
+        low_accs = {1: sum_tiles(1), 2: sum_tiles(1)}
+        gather_sum(own_acc, 0, [cen_t], None)
+        gather_sum(low_accs[1], 0, near, near_gates)
+        for n in range(PAIR):
+            gather_sum(low_accs[2], n, far, far_gates)
+        gather_sum(own_acc, 1, [cen_t], None)
+        gather_sum(low_accs[1], 1, near, near_gates)
+        own_back = banks.tile([P, V], F32, name="own_back", tag="e")
+        turn_back(own_acc, 0, [own_back[:, cols] for cols in halves], "own")
+        nc.scalar.copy(words_of(z_bf[0][:])[:, :, 0], own_back[:])
+
+        for z, lists, gates, tags in ((1, near, near_gates, "ab"), (2, far, far_gates, "cd")):
+            back = [banks.tile([P, PACK // PAIR, P], F32, name="back%d%d" % (z, u), tag=tags[u]) for u in range(HALVES)]
+            for a in range(PACK // PAIR):
+                if a == 0:
+                    accs = low_accs[z]
+                else:
+                    accs = sum_tiles(z)
+                    for i in range(PAIR):
+                        gather_sum(accs, PAIR * a + i, lists, gates)
+                turn_back(accs, a, [held[:, a, :] for held in back], "z%d" % z)
+            for u, cols in enumerate(halves):
+                nc.scalar.copy(words_of(z_bf[z][:, cols, :]), back[u][:].rearrange("p a v -> p v a"))
+
+        own = ring.tile([P, PAIR, V], BF16, name="own", tag="picked", align_bytes=64)
+        for s in range(PAIR):
+            nc.vector.tensor_copy(own[:, s, :], h[PAIR + s][:].indirect(cen_t[:]))
+        z1_q = quantize(z_bf[1][:].rearrange("p v t -> p (v t)"), "z1", ring, "picked")
+        nc.vector.tensor_copy(z_bf[0][:, :, PAIR:], own[:].rearrange("p s v -> p v s"))
+
+        def last_pass(result, i, codes, plane, start, stop):
+            nc.tensor.matmul_mx(
+                out=result[:], lhsT=w_words[i][:].bitcast(FP8X4), lhsT_scale=w_planes[i][:],
+                rhs=codes.bitcast(FP8X4), rhs_scale=plane, start=start, stop=stop,
             )
-            for n, (i, codes, plane) in enumerate(passes):
-                nc.tensor.matmul_mx(
-                    out=result[:], lhsT=w_words[i][:].bitcast(FP8X4), lhsT_scale=w_planes[i][:],
-                    rhs=codes.bitcast(FP8X4), rhs_scale=plane, start=(n == 0), stop=(n == len(passes) - 1),
-                )
+
+        results = [banks.tile([P, P], F32, name="result%d" % u, tag="cd"[u]) for u in range(HALVES)]
+        for u, cols in enumerate(halves):
+            last_pass(results[u], 1, z1_q[0][:, cols], z1_q[1][:, cols], True, False)
+            for z in (0, 2):
+                codes, plane = quantize(z_bf[z][:, cols, :].rearrange("p v t -> p (v t)"), "z%d_%d" % (z, u))
+                last_pass(results[u], z, codes[:], plane[:], False, z == 2)
             staged = keep.tile([P, P], F32, name="staged%d" % u)
-            nc.scalar.activation(staged[:], result[:], ACT.Tanh)
+            nc.scalar.activation(staged[:], results[u][:], ACT.Tanh)
             nc.sync.dma_start(out[:, cols], staged[:])

@@ -63,10 +63,6 @@ def tile_picked_zmix_tanh_p_kernel(
 
         x_plane = keep.tile([P, T], U8, name="x_plane", align_bytes=64)
         nc.gpsimd.memset(x_plane[:].bitcast(I32), 0)
-        warm_in = keep.tile([P, 1], F32, name="warm_in")
-        warm_out = keep.tile([P, 1], F32, name="warm_out")
-        nc.vector.memset(warm_in[:], 0.0)
-        nc.scalar.activation(warm_out[:], warm_in[:], ACT.Tanh)
 
         load_w1(0, slice(0, PAIR))
         offs_t = load_list(offs, "offs_t")

@@ -18,9 +18,9 @@ MULT = mybir.AluOpType.mult
 
 P = 128
 PACK = 4
-HALVES = V // P
 PAIR = 2
-Q = P // 2
+HALVES = V // P
+QUAD = P // 4
 PICKED_BUFS = 4
 
 
@@ -32,17 +32,17 @@ def tile_picked_zmix_tanh_p_kernel(
     with ExitStack() as ctx:
         keep = ctx.enter_context(tc.tile_pool(name="keep", bufs=1))
         ring = ctx.enter_context(tc.tile_pool(name="ring", bufs=PICKED_BUFS))
+        shared = ctx.enter_context(tc.tile_pool(name="shared", bufs=1))
         banks = ctx.enter_context(tc.psum_pool(name="banks", bufs=1))
-        sums = ctx.enter_context(tc.psum_pool(name="sums", bufs=3))
 
         def load_list(src, name):
             held = keep.tile(list(src.shape), U16, name=name)
             nc.sync.dma_start(held[:], src)
             return held
 
-        def load_scale_rows(plane, scales):
+        def load_scale_rows(plane, scales, queues=(nc.sync,) * 4):
             for q in range(4):
-                nc.sync.dma_start(plane[32 * q : 32 * q + 4, :].bitcast(I32), scales[0, 4 * q : 4 * q + 4, :].bitcast(I32))
+                queues[q].dma_start(plane[32 * q : 32 * q + 4, :].bitcast(I32), scales[0, 4 * q : 4 * q + 4, :].bitcast(I32))
 
         def load_words(words, name):
             held = keep.tile([P, words.shape[2]], I32, name=name, align_bytes=64)
@@ -50,35 +50,34 @@ def tile_picked_zmix_tanh_p_kernel(
             return held
 
         def load_gates(weights, name):
-            held = keep.tile([P, D, V], F32, name=name)
+            held = keep.tile([P, weights.shape[0], V], F32, name=name)
             nc.sync.dma_start(held[:], weights.rearrange("d p v -> p d v"))
-            return held
+            return [held[:, d, :] for d in range(weights.shape[0])]
 
         w1_rows = w1.rearrange("(p j) c -> p j c", j=PACK)
-
-        w1_raw = [keep.tile([P, PACK, H // 2], F32, name="w1_raw%d" % half) for half in range(2)]
-
-        def load_w1(half, rows):
-            nc.sync.dma_start(w1_raw[half][:, rows, :], w1_rows[:, rows, half * H // 2 : (half + 1) * H // 2])
 
         x_plane = keep.tile([P, T], U8, name="x_plane", align_bytes=64)
         nc.gpsimd.memset(x_plane[:].bitcast(I32), 0)
 
-        load_w1(0, slice(0, PAIR))
+        row_pairs = [slice(0, PAIR), slice(PAIR, PACK)]
+        first_raw = keep.tile([P, PACK, P], F32, name="first_raw")
+        nc.sync.dma_start(first_raw[:, row_pairs[0], :], w1_rows[:, row_pairs[0], :P])
         offs_t = load_list(offs, "offs_t")
-        load_scale_rows(x_plane, x_scales)
+        load_scale_rows(x_plane, x_scales, (nc.sync, nc.scalar, nc.sync, nc.scalar))
+        nc.sync.dma_start(first_raw[:, row_pairs[1], :], w1_rows[:, row_pairs[1], :P])
+        w1_first = first_raw[:].rearrange("p j (q t) -> p q j t", t=PACK)
         x_table = load_words(x_words, "x_table")
-        load_w1(0, slice(PAIR, PACK))
-        cen_t = load_list(cen, "cen_t")
-        gate_cols = keep.tile([P, D * HALVES], F32, name="gate_cols")
-        half_rows = gate.rearrange("d r (u p) -> (d r u) p", p=P)
-        with nc.allow_non_contiguous_dma(reason="one gate value a partition"):
-            nc.sync.dma_start(gate_cols[:], half_rows[:: P + 1, :].rearrange("i p -> p i"))
+        first_gate = load_gates(gate[:1], "first_gate")
         near = [load_list(src, "near%d" % d) for d, src in enumerate((pos1, pos2, pos3))]
-        load_w1(1, slice(0, PACK))
-        w1_a, w1_b = [raw[:].rearrange("p j (q t) -> p q j t", t=PACK) for raw in w1_raw]
+        rest_raw = shared.tile([P, PACK, H - P], F32, name="rest_raw", offset=0)
+        nc.sync.dma_start(rest_raw[:, :, P:], w1_rows[:, :, 2 * P :])
+        w1_rest = rest_raw[:].rearrange("p j (q t) -> p q j t", t=PACK)
+        w1_second, w1_upper = w1_rest[:, :QUAD, :, :], w1_rest[:, QUAD:, :, :]
+        later_gates = load_gates(gate[1:], "later_gates")
         far = [load_list(src, "far%d" % d) for d, src in enumerate((far1, far2, far3))]
         far_gates = load_gates(gate2, "far_gates")
+        nc.sync.dma_start(rest_raw[:, :, :P], w1_rows[:, :, P : 2 * P])
+        cen_t = load_list(cen, "cen_t")
 
         ident = keep.tile([P, P], F32, name="ident")
         make_identity(nc, ident[:])
@@ -94,141 +93,165 @@ def tile_picked_zmix_tanh_p_kernel(
         def quantize(values, name, pool=keep, tag=None):
             width = values.shape[1] // PACK
             codes = pool.tile([P, width], U32, name=name + "_codes", tag=tag or name + "_codes", align_bytes=64)
-            plane = keep.tile([P, width], U8, name=name + "_plane", align_bytes=64)
+            plane = keep.tile([P, width], U8, name=name + "_plane", tag=name + "_plane", align_bytes=64)
             nc.vector.quantize_mx(out=codes[:].bitcast(FP8X4), scales=plane[:], in_=values)
-            return codes, plane
+            return codes[:], plane[:]
 
-        first = keep.tile([P, 2, Q, PACK], BF16, name="first", tag="first", align_bytes=64)
-        second = keep.tile([P, 2, Q, PACK], BF16, name="second", tag="second", align_bytes=64)
-        high = keep.tile([P, PAIR, 2, Q, PACK], BF16, name="high", tag="high", align_bytes=64)
-        for rows in (slice(0, PAIR), slice(PAIR, PACK)):
-            nc.scalar.copy(first[:, :, :, rows].rearrange("p s q j -> p q j s"), w1_a[:, :, rows, :PAIR])
-        nc.scalar.copy(high[:, :, 0, :, :].rearrange("p s q j -> p q j s"), w1_a[:, :, :, PAIR:])
-        nc.scalar.copy(second[:].rearrange("p s q j -> p q j s"), w1_b[:, :, :, :PAIR])
-        nc.scalar.copy(high[:, :, 1, :, :].rearrange("p s q j -> p q j s"), w1_b[:, :, :, PAIR:])
-        w1_bf = [low[:].rearrange("p a q j -> p (a q j)") for low in (first, second)]
+        halves = [slice(u * P, (u + 1) * P) for u in range(HALVES)]
+        node_halves = [slice(0, S // 2), slice(S // 2, S)]
+        pieces = [slice(0, 256), slice(256, 384), slice(384, S)]
+
+        rounded_first = keep.tile([P, PACK, QUAD, PACK], BF16, name="rounded_first", align_bytes=64)
+        for rows in row_pairs:
+            nc.scalar.copy(rounded_first[:, :, :, rows].rearrange("p t q j -> p q j t"), w1_first[:, :, rows, :])
 
         x_scale = keep.tile([P, S], U8, name="x_scale", align_bytes=64)
         nc.vector.tensor_copy(x_scale[:], x_plane[:].indirect(offs_t[:]))
-        x_codes = keep.tile([P, S], U32, name="x_codes", align_bytes=64)
-        nc.vector.tensor_copy(x_codes[:], x_table[:].bitcast(U32).indirect(offs_t[:]))
-        first_q = quantize(w1_bf[0], "w1_0")
+        first_q = quantize(rounded_first[:].rearrange("p t q j -> p (t q j)"), "w1_first", tag="chain")
+        x_codes = {}
+        for b, cols in enumerate(pieces):
+            held = keep.tile([P, cols.stop - cols.start], U32, name="x_codes%d" % b, tag="words%d" % b, align_bytes=64)
+            nc.vector.tensor_copy(held[:], x_table[:].bitcast(U32).indirect(offs_t[:, cols.start // 16 : cols.stop // 16]))
+            x_codes[cols.start] = held
 
-        h = []
+        def product(acc, weights, cols):
+            nc.tensor.matmul_mx(
+                out=acc, lhsT=weights[0].bitcast(FP8X4), lhsT_scale=weights[1],
+                rhs=x_codes[cols.start][:].bitcast(FP8X4), rhs_scale=x_scale[:, cols],
+                start=True, stop=True,
+            )
 
-        def make_h(codes, plane):
-            n = len(h)
-            h_n = keep.tile([P, S], F32, name="h%d" % n)
-
-            def product(acc, cols):
-                nc.tensor.matmul_mx(
-                    out=acc, lhsT=codes[:].bitcast(FP8X4), lhsT_scale=plane[:],
-                    rhs=x_codes[:, cols].bitcast(FP8X4), rhs_scale=x_scale[:, cols], start=True, stop=True,
-                )
-
-            if n == 0:
-                for cols, bank in zip((slice(0, 256), slice(256, 384), slice(384, S)), "ade"):
-                    acc = banks.tile([P, cols.stop - cols.start], F32, name="h_part%d" % cols.start, tag=bank)
-                    product(acc[:], cols)
-                    if cols.start == 0:
-                        nc.vector.tensor_relu(h_n[:, cols], acc[:])
-                    else:
-                        nc.scalar.activation(h_n[:, cols], acc[:], ACT.Relu)
-            elif n == 1:
-                for cols, bank in zip((slice(0, 256), slice(256, S)), "be"):
-                    acc = banks.tile([P, S // 2], F32, name="h_half%d" % cols.start, tag=bank)
-                    product(acc[:], cols)
+        def make_h(name, weights, parts, h_n=None):
+            if h_n is None:
+                h_n = keep.tile([P, S], F32, name=name)
+            for cols, bank, on_vector in parts:
+                acc = banks.tile([P, cols.stop - cols.start], F32, name="%s_%d" % (name, cols.start), tag=bank)
+                for part in pieces:
+                    if cols.start <= part.start and part.stop <= cols.stop:
+                        product(acc[:, part.start - cols.start : part.stop - cols.start], weights, part)
+                if on_vector:
+                    nc.vector.tensor_relu(h_n[:, cols], acc[:])
+                else:
                     nc.scalar.activation(h_n[:, cols], acc[:], ACT.Relu)
-            else:
-                acc = banks.tile([P, S], F32, name="h_acc%d" % n, tag="abcd"[n])
-                product(acc[:], slice(0, S))
-                nc.scalar.activation(h_n[:], acc[:], ACT.Relu)
-            h.append(h_n)
+            return h_n
 
-        make_h(*first_q)
-        near_gates = keep.tile([P, D, V], F32, name="near_gates")
-        for d in range(D):
-            spread = sums.tile([P, HALVES, P], F32, name="spread%d" % d, tag="acc")
-            for u in range(HALVES):
-                column = gate_cols[:, HALVES * d + u : HALVES * d + u + 1]
-                nc.tensor.transpose(spread[:, u, :], column.to_broadcast([P, P]), ident[:])
-            nc.scalar.copy(near_gates[:, d, :], spread[:].rearrange("p u v -> p (u v)"))
-        make_h(*quantize(w1_bf[1], "w1_1"))
-        codes, plane = quantize(high[:].rearrange("p s a q j -> p (s a q j)"), "w1_high")
+        h_first = make_h("h_first", first_q, [(pieces[0], "a", False), (pieces[1], "d", False), (pieces[2], "e", False)])
+        rounded_upper = keep.tile([P, PAIR, 2 * QUAD, PACK], BF16, name="rounded_upper", tag="chain", align_bytes=64)
+        nc.scalar.copy(rounded_upper[:].rearrange("p s q j -> p q j s"), w1_upper[:, :, :, :PAIR])
+        upper_q = quantize(rounded_upper[:].rearrange("p s q j -> p (s q j)"), "w1_upper")
+        rounded_mixed = keep.tile([P, PAIR, P, PACK], BF16, name="rounded_mixed", tag="w1_first_plane", align_bytes=64)
+        nc.scalar.copy(rounded_mixed[:, :, 2 * QUAD :, :].rearrange("p i q j -> p q j i"), w1_upper[:, :, :, PAIR:])
+        nc.scalar.copy(
+            rounded_mixed[:, :, : 2 * QUAD, :].rearrange("p i (a q) j -> p q j a i", a=2),
+            w1_second.rearrange("p q j (a i) -> p q j a i", a=2),
+        )
+        codes, plane = quantize(rounded_mixed[:].rearrange("p i m j -> p (i m j)"), "w1_mixed")
+        h_upper = make_h(
+            "h_upper", upper_q, [(node_halves[0], "b", False), (node_halves[1], "e", False)],
+            shared.tile([P, S], F32, name="h_upper", offset=4096),
+        )
+        h_mixed = [
+            make_h("h_mixed%d" % i, (codes[:, halves[i]], plane[:, halves[i]]), [(slice(0, S), "ad"[i], False)]) for i in range(PAIR)
+        ]
+        own_low = keep.tile([P, S], F32, name="own_low")
+        own_high = [keep.tile([P, S], F32, name="own_high%d" % i) for i in range(PAIR)]
         for s in range(PAIR):
-            make_h(codes[:, s * P : (s + 1) * P], plane[:, s * P : (s + 1) * P])
+            nc.sync.dma_start(own_low[64 * s : 64 * s + 32, :], h_first[32 * s : 32 * s + 32, :])
+            nc.sync.dma_start(own_high[s][:32, :], h_first[64 + 32 * s : 96 + 32 * s, :])
+        for s in range(PAIR):
+            nc.sync.dma_start(own_low[64 * s + 32 : 64 * s + 64, :], h_mixed[s][:32, :])
+            nc.sync.dma_start(own_high[s][32:64, :], h_mixed[s][32:64, :])
+            nc.sync.dma_start(own_high[s][64:, :], h_mixed[s][64:, :])
 
-        def gather_sum(accs, n, lists, gates):
-            i = n % PAIR
+        def gather_sum(window, lists, gates, targets, opens, closes, split_last=False):
             for d, held in enumerate(lists):
                 picked = ring.tile([P, V], F32, name="picked", align_bytes=64)[:]
                 if gates is None:
-                    nc.vector.tensor_copy(picked, h[n][:].indirect(held[:]))
-                elif len(accs) == HALVES and i == PAIR - 1 and d == D - 1:
+                    nc.vector.tensor_copy(picked, window[:].indirect(held[:]))
+                elif split_last and d == D - 1:
                     for cols in halves:
-                        window = h[n][:].indirect(held[:, cols.start // 16 : cols.stop // 16])
-                        nc.vector.tensor_tensor(picked[:, cols], window, gates[:, d, cols], MULT)
+                        part = window[:].indirect(held[:, cols.start // 16 : cols.stop // 16])
+                        nc.vector.tensor_tensor(picked[:, cols], part, gates[d][:, cols], MULT)
                 else:
-                    nc.vector.tensor_tensor(picked, h[n][:].indirect(held[:]), gates[:, d, :], MULT)
-                per_bank = HALVES // len(accs)
-                for u in range(HALVES):
+                    nc.vector.tensor_tensor(picked, window[:].indirect(held[:]), gates[d], MULT)
+                for u, cols in enumerate(halves):
                     nc.tensor.matmul(
-                        accs[u // per_bank][:, u % per_bank, i, :], lhsT=picked[:, u * P : (u + 1) * P], rhs=ident[:], is_transpose=True,
-                        start=(d == 0 and i == 0 and u % per_bank == 0),
-                        stop=(d == len(lists) - 1 and i == PAIR - 1 and u % per_bank == per_bank - 1),
+                        targets[u], lhsT=picked[:, cols], rhs=ident[:], is_transpose=True,
+                        start=(d == 0 and u in opens), stop=(d == len(lists) - 1 and u in closes),
                     )
 
-        def turn_back(accs, a, backs, name):
-            per_bank = HALVES // len(accs)
-            for b, acc in enumerate(accs):
-                rounded = keep.tile([P, per_bank, P, PAIR], BF16, name="rounded%s%d%d" % (name, a, b))
-                if a == 0:
-                    nc.scalar.copy(
-                        rounded[:].rearrange("v u (i q) s -> v u i q s", i=PAIR), acc[:].rearrange("v u i (s q) -> v u i q s", s=PAIR)
-                    )
-                else:
-                    nc.scalar.copy(rounded[:], acc[:].rearrange("v u s p -> v u p s"))
-                for u in range(per_bank):
-                    words = rounded[:, u, :, :].rearrange("v p s -> v (p s)").bitcast(F32)
-                    nc.tensor.transpose(backs[b * per_bank + u], words, ident[:])
-
-        def sum_tiles(count):
-            return [sums.tile([P, HALVES // count, PAIR, P], F32, name="acc", tag="acc") for b in range(count)]
+        pairs = {
+            z: [shared.tile([P, PAIR, P, PAIR], BF16, name="pairs%d%d" % (z, u), offset=1024 * (HALVES * (z - 1) + u)) for u in range(HALVES)]
+            for z in (1, 2)
+        }
+        z_bf = [keep.tile([P, V, PACK], BF16, name="z_bf%d" % z, align_bytes=64) for z in range(3)]
 
         def words_of(values):
             return values.rearrange("p v t -> p (v t)").bitcast(F32).rearrange("p (v a) -> p v a", a=PACK // PAIR)
 
-        halves = [slice(u * P, (u + 1) * P) for u in range(HALVES)]
-        z_bf = [keep.tile([P, V, PACK], BF16, name="z_bf%d" % z, align_bytes=64) for z in range(3)]
+        def turn_back(target, values):
+            nc.tensor.transpose(target, values.rearrange("v p s -> v (p s)").bitcast(F32), ident[:])
 
-        own_acc = sum_tiles(1)
-        low_accs = {1: sum_tiles(1), 2: sum_tiles(1)}
-        gather_sum(own_acc, 0, [cen_t], None)
-        gather_sum(low_accs[1], 0, near, near_gates)
-        for n in range(PAIR):
-            gather_sum(low_accs[2], n, far, far_gates)
-        gather_sum(own_acc, 1, [cen_t], None)
-        gather_sum(low_accs[1], 1, near, near_gates)
-        own_back = banks.tile([P, V], F32, name="own_back", tag="e")
-        turn_back(own_acc, 0, [own_back[:, cols] for cols in halves], "own")
+        def round_upper(z, u, acc):
+            nc.scalar.copy(pairs[z][u][:, 0, 2 * QUAD :, :], acc.rearrange("v (s q) -> v q s", s=PAIR))
+
+        def round_mixed(z, acc):
+            for u in range(HALVES):
+                nc.scalar.copy(pairs[z][u][:, 1, QUAD:, :], acc[:, u, :, QUAD:].rearrange("v i m -> v m i"))
+                nc.scalar.copy(pairs[z][u][:, 0, QUAD : 2 * QUAD, :], acc[:, u, :, :QUAD].rearrange("v i m -> v m i"))
+
+        sets = {1: (near, first_gate + later_gates), 2: (far, far_gates)}
+
+        acc = banks.tile([P, 2, HALVES, P], F32, name="first_sums", tag="x")
+        gather_sum(h_first, *sets[1], [acc[:, 0, u, :] for u in range(HALVES)], (0,), ())
+        gather_sum(h_first, *sets[2], [acc[:, 1, u, :] for u in range(HALVES)], (), (1,))
+        for z in (1, 2):
+            for u in range(HALVES):
+                nc.scalar.copy(pairs[z][u][:, :, :QUAD, :], acc[:, z - 1, u, :].rearrange("v (a s q) -> v a q s", a=2, s=PAIR))
+
+        acc = banks.tile([P, HALVES, P], F32, name="upper_near", tag="y")
+        gather_sum(h_upper, *sets[1], [acc[:, u, :] for u in range(HALVES)], (0,), (1,))
+        for u in range(HALVES):
+            round_upper(1, u, acc[:, u, :])
+        own_acc = banks.tile([P, HALVES, PAIR, P], F32, name="own_acc", tag="e")
+        gather_sum(h_upper, [cen_t], None, [own_acc[:, u, 1, :] for u in range(HALVES)], (0,), ())
+
+        acc = banks.tile([P, HALVES, PAIR, P], F32, name="mixed_near", tag="z")
+        for i in range(PAIR):
+            gather_sum(h_mixed[i], *sets[1], [acc[:, u, i, :] for u in range(HALVES)], (0,) if i == 0 else (), (1,) if i == 1 else ())
+        round_mixed(1, acc)
+        back = banks.tile([P, HALVES, PAIR, P], F32, name="near_back", tag="b")
+        for u in range(HALVES):
+            for a in range(PAIR):
+                turn_back(back[:, u, a, :], pairs[1][u][:, a, :, :])
+        nc.scalar.copy(words_of(z_bf[1][:]).rearrange("p (u v) a -> p u v a", u=HALVES), back[:].rearrange("p u a v -> p u v a"))
+
+        gather_sum(own_low, [cen_t], None, [own_acc[:, u, 0, :] for u in range(HALVES)], (), (1,))
+        own_pairs = keep.tile([P, HALVES, P, PAIR], BF16, name="own_pairs")
+        nc.scalar.copy(own_pairs[:].rearrange("v u (i q) s -> v u i q s", i=PAIR), own_acc[:].rearrange("v u i (s q) -> v u i q s", s=PAIR))
+        own_back = banks.tile([P, V], F32, name="own_back", tag="y")
+        for u, cols in enumerate(halves):
+            turn_back(own_back[:, cols], own_pairs[:, u, :, :])
         nc.scalar.copy(words_of(z_bf[0][:])[:, :, 0], own_back[:])
 
-        for z, lists, gates, tags in ((1, near, near_gates, "ab"), (2, far, far_gates, "cd")):
-            back = [banks.tile([P, PACK // PAIR, P], F32, name="back%d%d" % (z, u), tag=tags[u]) for u in range(HALVES)]
-            for a in range(PACK // PAIR):
-                if a == 0:
-                    accs = low_accs[z]
-                else:
-                    accs = sum_tiles(z)
-                    for i in range(PAIR):
-                        gather_sum(accs, PAIR * a + i, lists, gates)
-                turn_back(accs, a, [held[:, a, :] for held in back], "z%d" % z)
-            for u, cols in enumerate(halves):
-                nc.scalar.copy(words_of(z_bf[z][:, cols, :]), back[u][:].rearrange("p a v -> p v a"))
+        acc = banks.tile([P, HALVES, PAIR, P], F32, name="mixed_far", tag="x")
+        for i in range(PAIR):
+            gather_sum(h_mixed[i], *sets[2], [acc[:, u, i, :] for u in range(HALVES)], (0,) if i == 0 else (), (1,) if i == 1 else ())
+        round_mixed(2, acc)
+        far_back = [banks.tile([P, PAIR, P], F32, name="far_back%d" % u, tag="cd"[u]) for u in range(HALVES)]
+        for u in range(HALVES):
+            turn_back(far_back[u][:, 1, :], pairs[2][u][:, 1, :, :])
 
+        accs = [banks.tile([P, P], F32, name="upper_far%d" % u, tag="za"[u]) for u in range(HALVES)]
+        gather_sum(h_upper, *sets[2], [held[:] for held in accs], (0, 1), (0, 1), split_last=True)
+        for u in range(HALVES):
+            round_upper(2, u, accs[u][:])
+            turn_back(far_back[u][:, 0, :], pairs[2][u][:, 0, :, :])
+        for u, cols in enumerate(halves):
+            nc.scalar.copy(words_of(z_bf[2][:, cols, :]), far_back[u][:].rearrange("p a v -> p v a"))
         own = ring.tile([P, PAIR, V], BF16, name="own", tag="picked", align_bytes=64)
         for s in range(PAIR):
-            nc.vector.tensor_copy(own[:, s, :], h[PAIR + s][:].indirect(cen_t[:]))
+            nc.vector.tensor_copy(own[:, s, :], own_high[s][:].indirect(cen_t[:]))
         z1_q = quantize(z_bf[1][:].rearrange("p v t -> p (v t)"), "z1", ring, "picked")
         nc.vector.tensor_copy(z_bf[0][:, :, PAIR:], own[:].rearrange("p s v -> p v s"))
 
@@ -243,7 +266,7 @@ def tile_picked_zmix_tanh_p_kernel(
             last_pass(results[u], 1, z1_q[0][:, cols], z1_q[1][:, cols], True, False)
             for z in (0, 2):
                 codes, plane = quantize(z_bf[z][:, cols, :].rearrange("p v t -> p (v t)"), "z%d_%d" % (z, u))
-                last_pass(results[u], z, codes[:], plane[:], False, z == 2)
+                last_pass(results[u], z, codes, plane, False, z == 2)
             staged = keep.tile([P, P], F32, name="staged%d" % u)
             nc.scalar.activation(staged[:], results[u][:], ACT.Tanh)
             nc.sync.dma_start(out[:, cols], staged[:])

@@ -108,16 +108,14 @@ def tile_picked_zmix_tanh_p_kernel(
         x_scale = keep.tile([P, S], U8, name="x_scale", align_bytes=64)
         nc.vector.tensor_copy(x_scale[:], x_plane[:].indirect(offs_t[:]))
         first_q = quantize(rounded_first[:].rearrange("p t q j -> p (t q j)"), "w1_first", tag="chain")
-        x_codes = {}
-        for b, cols in enumerate(pieces):
-            held = keep.tile([P, cols.stop - cols.start], U32, name="x_codes%d" % b, tag="words%d" % b, align_bytes=64)
-            nc.vector.tensor_copy(held[:], x_table[:].bitcast(U32).indirect(offs_t[:, cols.start // 16 : cols.stop // 16]))
-            x_codes[cols.start] = held
+        x_codes = keep.tile([P, S], U32, name="x_codes", align_bytes=64)
+        for cols in pieces:
+            nc.vector.tensor_copy(x_codes[:, cols], x_table[:].bitcast(U32).indirect(offs_t[:, cols.start // 16 : cols.stop // 16]))
 
         def product(acc, weights, cols):
             nc.tensor.matmul_mx(
                 out=acc, lhsT=weights[0].bitcast(FP8X4), lhsT_scale=weights[1],
-                rhs=x_codes[cols.start][:].bitcast(FP8X4), rhs_scale=x_scale[:, cols],
+                rhs=x_codes[:, cols].bitcast(FP8X4), rhs_scale=x_scale[:, cols],
                 start=True, stop=True,
             )
 
@@ -126,9 +124,7 @@ def tile_picked_zmix_tanh_p_kernel(
                 h_n = keep.tile([P, S], F32, name=name)
             for cols, bank, on_vector in parts:
                 acc = banks.tile([P, cols.stop - cols.start], F32, name="%s_%d" % (name, cols.start), tag=bank)
-                for part in pieces:
-                    if cols.start <= part.start and part.stop <= cols.stop:
-                        product(acc[:, part.start - cols.start : part.stop - cols.start], weights, part)
+                product(acc[:], weights, cols)
                 if on_vector:
                     nc.vector.tensor_relu(h_n[:, cols], acc[:])
                 else:

@@ -67,10 +67,10 @@ def tile_picked_zmix_tanh_p_kernel(
         nc.sync.dma_start(first_raw[:, row_pairs[1], :], w1_rows[:, row_pairs[1], :P])
         w1_first = first_raw[:].rearrange("p j (q t) -> p q j t", t=PACK)
         x_table = load_words(x_words, "x_table")
-        first_gate = load_gates(gate[:1], "first_gate")
-        near = [load_list(src, "near%d" % d) for d, src in enumerate((pos1, pos2, pos3))]
         rest_raw = shared.tile([P, PACK, H - P], F32, name="rest_raw", offset=0)
         nc.sync.dma_start(rest_raw[:, :, P:], w1_rows[:, :, 2 * P :])
+        first_gate = load_gates(gate[:1], "first_gate")
+        near = [load_list(src, "near%d" % d) for d, src in enumerate((pos1, pos2, pos3))]
         w1_rest = rest_raw[:].rearrange("p j (q t) -> p q j t", t=PACK)
         w1_second, w1_upper = w1_rest[:, :QUAD, :, :], w1_rest[:, QUAD:, :, :]
         later_gates = load_gates(gate[1:], "later_gates")
@@ -132,8 +132,8 @@ def tile_picked_zmix_tanh_p_kernel(
             return h_n
 
         h_first = make_h("h_first", first_q, [(pieces[0], "a", False), (pieces[1], "d", False), (pieces[2], "e", False)])
-        rounded_upper = keep.tile([P, PAIR, 2 * QUAD, PACK], BF16, name="rounded_upper", tag="chain", align_bytes=64)
-        nc.scalar.copy(rounded_upper[:].rearrange("p s q j -> p q j s"), w1_upper[:, :, :, :PAIR])
+        rounded_upper = keep.tile([P, PAIR, 2 * QUAD, PACK], BF16, name="rounded_upper", align_bytes=64)
+        nc.vector.tensor_copy(rounded_upper[:].rearrange("p s q j -> p q j s"), w1_upper[:, :, :, :PAIR])
         upper_q = quantize(rounded_upper[:].rearrange("p s q j -> p (s q j)"), "w1_upper")
         rounded_mixed = keep.tile([P, PAIR, P, PACK], BF16, name="rounded_mixed", tag="w1_first_plane", align_bytes=64)
         nc.scalar.copy(rounded_mixed[:, :, 2 * QUAD :, :].rearrange("p i q j -> p q j i"), w1_upper[:, :, :, PAIR:])
@@ -222,6 +222,8 @@ def tile_picked_zmix_tanh_p_kernel(
                 turn_back(back[:, u, a, :], pairs[1][u][:, a, :, :])
         nc.scalar.copy(words_of(z_bf[1][:]).rearrange("p (u v) a -> p u v a", u=HALVES), back[:].rearrange("p u a v -> p u v a"))
 
+        acc = banks.tile([P, HALVES, PAIR, P], F32, name="mixed_far", tag="x")
+        gather_sum(h_mixed[0], *sets[2], [acc[:, u, 0, :] for u in range(HALVES)], (0,), ())
         gather_sum(own_low, [cen_t], None, [own_acc[:, u, 0, :] for u in range(HALVES)], (), (1,))
         own_pairs = keep.tile([P, HALVES, P, PAIR], BF16, name="own_pairs")
         nc.scalar.copy(own_pairs[:].rearrange("v u (i q) s -> v u i q s", i=PAIR), own_acc[:].rearrange("v u i (s q) -> v u i q s", s=PAIR))
@@ -230,9 +232,7 @@ def tile_picked_zmix_tanh_p_kernel(
             turn_back(own_back[:, cols], own_pairs[:, u, :, :])
         nc.scalar.copy(words_of(z_bf[0][:])[:, :, 0], own_back[:])
 
-        acc = banks.tile([P, HALVES, PAIR, P], F32, name="mixed_far", tag="x")
-        for i in range(PAIR):
-            gather_sum(h_mixed[i], *sets[2], [acc[:, u, i, :] for u in range(HALVES)], (0,) if i == 0 else (), (1,) if i == 1 else ())
+        gather_sum(h_mixed[1], *sets[2], [acc[:, u, 1, :] for u in range(HALVES)], (), (1,))
         round_mixed(2, acc)
         far_back = [banks.tile([P, PAIR, P], F32, name="far_back%d" % u, tag="cd"[u]) for u in range(HALVES)]
         for u in range(HALVES):
@@ -248,8 +248,18 @@ def tile_picked_zmix_tanh_p_kernel(
         own = ring.tile([P, PAIR, V], BF16, name="own", tag="picked", align_bytes=64)
         for s in range(PAIR):
             nc.vector.tensor_copy(own[:, s, :], own_high[s][:].indirect(cen_t[:]))
-        z1_q = quantize(z_bf[1][:].rearrange("p v t -> p (v t)"), "z1", ring, "picked")
+        z1_codes = ring.tile([P, V], U32, name="z1_codes", tag="picked", align_bytes=64)
+        z1_plane = keep.tile([P, V], U8, name="z1_plane", align_bytes=64)
+
+        def flat(z, cols):
+            return z_bf[z][:, cols, :].rearrange("p v t -> p (v t)")
+
+        def quantize_z1(cols):
+            nc.vector.quantize_mx(out=z1_codes[:, cols].bitcast(FP8X4), scales=z1_plane[:, cols], in_=flat(1, cols))
+
+        quantize_z1(halves[0])
         nc.vector.tensor_copy(z_bf[0][:, :, PAIR:], own[:].rearrange("p s v -> p v s"))
+        quantize_z1(halves[1])
 
         def last_pass(result, i, codes, plane, start, stop):
             nc.tensor.matmul_mx(
@@ -257,12 +267,14 @@ def tile_picked_zmix_tanh_p_kernel(
                 rhs=codes.bitcast(FP8X4), rhs_scale=plane, start=start, stop=stop,
             )
 
-        results = [banks.tile([P, P], F32, name="result%d" % u, tag="cd"[u]) for u in range(HALVES)]
+        results = [banks.tile([P, P], F32, name="result%d" % u, tag="ac"[u]) for u in range(HALVES)]
         for u, cols in enumerate(halves):
-            last_pass(results[u], 1, z1_q[0][:, cols], z1_q[1][:, cols], True, False)
-            for z in (0, 2):
-                codes, plane = quantize(z_bf[z][:, cols, :].rearrange("p v t -> p (v t)"), "z%d_%d" % (z, u))
-                last_pass(results[u], z, codes, plane, False, z == 2)
+            last_pass(results[u], 1, z1_codes[:, cols], z1_plane[:, cols], True, False)
+            codes, plane = quantize(flat(0, cols), "z0_%d" % u)
+            last_pass(results[u], 0, codes, plane, False, False)
+        for u, cols in enumerate(halves):
+            codes, plane = quantize(flat(2, cols), "z2_%d" % u)
+            last_pass(results[u], 2, codes, plane, False, True)
             staged = keep.tile([P, P], F32, name="staged%d" % u)
             nc.scalar.activation(staged[:], results[u][:], ACT.Tanh)
             nc.sync.dma_start(out[:, cols], staged[:])

@@ -59,7 +59,7 @@ def tile_picked_zmix_tanh_p_kernel(
         x_plane = keep.tile([P, T], U8, name="x_plane", align_bytes=64)
         nc.gpsimd.memset(x_plane[:].bitcast(I32), 0)
 
-        row_pairs = [slice(0, PAIR), slice(PAIR, PACK)]
+        row_pairs = [slice(0, PACK - 1), slice(PACK - 1, PACK)]
         first_raw = keep.tile([P, PACK, P], F32, name="first_raw")
         nc.sync.dma_start(first_raw[:, row_pairs[0], :], w1_rows[:, row_pairs[0], :P])
         offs_t = load_list(offs, "offs_t")
@@ -74,9 +74,11 @@ def tile_picked_zmix_tanh_p_kernel(
         w1_rest = rest_raw[:].rearrange("p j (q t) -> p q j t", t=PACK)
         w1_second, w1_upper = w1_rest[:, :QUAD, :, :], w1_rest[:, QUAD:, :, :]
         later_gates = load_gates(gate[1:], "later_gates")
-        far = [load_list(src, "far%d" % d) for d, src in enumerate((far1, far2, far3))]
-        far_gates = load_gates(gate2, "far_gates")
+        far_gates = load_gates(gate2[: D - 1], "far_gates")
+        far = [load_list(far1, "far0")]
         nc.sync.dma_start(rest_raw[:, :, :P], w1_rows[:, :, P : 2 * P])
+        far = far + [load_list(far2, "far1"), load_list(far3, "far2")]
+        far_gates = far_gates + load_gates(gate2[D - 1 :], "last_far_gate")
         cen_t = load_list(cen, "cen_t")
 
         ident = keep.tile([P, P], F32, name="ident")
@@ -134,14 +136,26 @@ def tile_picked_zmix_tanh_p_kernel(
         h_first = make_h("h_first", first_q, [(pieces[0], "a", False), (pieces[1], "d", False), (pieces[2], "e", False)])
         rounded_upper = keep.tile([P, PAIR, 2 * QUAD, PACK], BF16, name="rounded_upper", align_bytes=64)
         nc.vector.tensor_copy(rounded_upper[:].rearrange("p s q j -> p q j s"), w1_upper[:, :, :, :PAIR])
+        rounded_mixed = keep.tile([P, PAIR, P, PACK], BF16, name="rounded_mixed", align_bytes=64)
+        nc.vector.tensor_copy(rounded_mixed[:, :, 2 * QUAD :, :].rearrange("p i q j -> p q j i"), w1_upper[:, :, :, PAIR:])
         upper_q = quantize(rounded_upper[:].rearrange("p s q j -> p (s q j)"), "w1_upper")
-        rounded_mixed = keep.tile([P, PAIR, P, PACK], BF16, name="rounded_mixed", tag="w1_first_plane", align_bytes=64)
-        nc.scalar.copy(rounded_mixed[:, :, 2 * QUAD :, :].rearrange("p i q j -> p q j i"), w1_upper[:, :, :, PAIR:])
+        codes = keep.tile([P, PAIR * P], U32, name="mixed_codes", align_bytes=64)
+        plane = keep.tile([P, PAIR * P], U8, name="mixed_plane", align_bytes=64)
+
+        def quantize_mixed(start):
+            for i in range(PAIR):
+                cols = slice(i * P + start, i * P + start + 2 * QUAD)
+                nc.vector.quantize_mx(
+                    out=codes[:, cols].bitcast(FP8X4), scales=plane[:, cols],
+                    in_=rounded_mixed[:, i, start : start + 2 * QUAD, :].rearrange("p m j -> p (m j)"),
+                )
+
+        quantize_mixed(2 * QUAD)
         nc.scalar.copy(
             rounded_mixed[:, :, : 2 * QUAD, :].rearrange("p i (a q) j -> p q j a i", a=2),
             w1_second.rearrange("p q j (a i) -> p q j a i", a=2),
         )
-        codes, plane = quantize(rounded_mixed[:].rearrange("p i m j -> p (i m j)"), "w1_mixed")
+        quantize_mixed(0)
         h_upper = make_h(
             "h_upper", upper_q, [(node_halves[0], "b", False), (node_halves[1], "e", False)],
             shared.tile([P, S], F32, name="h_upper", offset=4096),

@@ -15,13 +15,15 @@ U8 = mybir.dt.uint8
 FP8X4 = mybir.dt.float8_e4m3fn_x4
 ACT = mybir.ActivationFunctionType
 MULT = mybir.AluOpType.mult
+ADD = mybir.AluOpType.add
 
 P = 128
 PACK = 4
 PAIR = 2
 HALVES = V // P
 QUAD = P // 4
-PICKED_BUFS = 4
+RING = 12
+H_BYTES = 4 * S
 
 
 def tile_picked_zmix_tanh_p_kernel(
@@ -31,7 +33,7 @@ def tile_picked_zmix_tanh_p_kernel(
     nc = tc.nc
     with ExitStack() as ctx:
         keep = ctx.enter_context(tc.tile_pool(name="keep", bufs=1))
-        ring = ctx.enter_context(tc.tile_pool(name="ring", bufs=PICKED_BUFS))
+        ring = ctx.enter_context(tc.tile_pool(name="ring", bufs=RING))
         shared = ctx.enter_context(tc.tile_pool(name="shared", bufs=1))
         banks = ctx.enter_context(tc.psum_pool(name="banks", bufs=1))
 
@@ -40,12 +42,8 @@ def tile_picked_zmix_tanh_p_kernel(
             nc.sync.dma_start(held[:], src)
             return held
 
-        def load_scale_rows(plane, scales, queues=(nc.sync,) * 4):
-            for q in range(4):
-                queues[q].dma_start(plane[32 * q : 32 * q + 4, :].bitcast(I32), scales[0, 4 * q : 4 * q + 4, :].bitcast(I32))
-
-        def load_words(words, name):
-            held = keep.tile([P, words.shape[2]], I32, name=name, align_bytes=64)
+        def load_words(words, name, pool=keep, offset=None):
+            held = pool.tile([P, words.shape[2]], I32, name=name, align_bytes=64, offset=offset)
             nc.sync.dma_start(held[:], words[0].rearrange("p n r -> p (n r)").bitcast(I32))
             return held
 
@@ -56,239 +54,256 @@ def tile_picked_zmix_tanh_p_kernel(
 
         w1_rows = w1.rearrange("(p j) c -> p j c", j=PACK)
 
-        x_plane = keep.tile([P, T], U8, name="x_plane", align_bytes=64)
-        nc.gpsimd.memset(x_plane[:].bitcast(I32), 0)
-
-        row_pairs = [slice(0, PACK - 1), slice(PACK - 1, PACK)]
+        row_parts = [slice(0, 1), slice(1, PACK)]
         first_raw = keep.tile([P, PACK, P], F32, name="first_raw")
-        nc.sync.dma_start(first_raw[:, row_pairs[0], :], w1_rows[:, row_pairs[0], :P])
+        nc.sync.dma_start(first_raw[:, row_parts[0], :], w1_rows[:, row_parts[0], :P])
         offs_t = load_list(offs, "offs_t")
-        load_scale_rows(x_plane, x_scales, (nc.sync, nc.scalar, nc.sync, nc.scalar))
-        nc.sync.dma_start(first_raw[:, row_pairs[1], :], w1_rows[:, row_pairs[1], :P])
-        w1_first = first_raw[:].rearrange("p j (q t) -> p q j t", t=PACK)
+        x_plane = keep.tile([P, T], U8, name="x_plane", align_bytes=64)
+        for q in range(4):
+            rows = x_scales[0, 4 * q : 4 * q + 4, :].bitcast(I32)
+            (nc.sync, nc.scalar)[q % 2].dma_start(x_plane[32 * q : 32 * q + 32, :].bitcast(I32), rows.unsqueeze(0).to_broadcast([8, 4, T // 4]))
+        nc.sync.dma_start(first_raw[:, row_parts[1], :], w1_rows[:, row_parts[1], :P])
         x_table = load_words(x_words, "x_table")
-        rest_raw = shared.tile([P, PACK, H - P], F32, name="rest_raw", offset=0)
-        nc.sync.dma_start(rest_raw[:, :, P:], w1_rows[:, :, 2 * P :])
-        first_gate = load_gates(gate[:1], "first_gate")
-        near = [load_list(src, "near%d" % d) for d, src in enumerate((pos1, pos2, pos3))]
-        w1_rest = rest_raw[:].rearrange("p j (q t) -> p q j t", t=PACK)
-        w1_second, w1_upper = w1_rest[:, :QUAD, :, :], w1_rest[:, QUAD:, :, :]
-        later_gates = load_gates(gate[1:], "later_gates")
-        far_gates = load_gates(gate2[: D - 1], "far_gates")
+        second_raw = shared.tile([P, PACK, P], F32, name="second_raw", align_bytes=64, offset=14 * H_BYTES)
+        nc.sync.dma_start(second_raw[:], w1_rows[:, :, P : 2 * P])
+        upper_raw = shared.tile([P, PACK, 2 * P], F32, name="upper_raw", align_bytes=64, offset=11 * H_BYTES)
+        nc.sync.dma_start(upper_raw[:], w1_rows[:, :, 2 * P :])
         far = [load_list(far1, "far0")]
-        nc.sync.dma_start(rest_raw[:, :, :P], w1_rows[:, :, P : 2 * P])
-        far = far + [load_list(far2, "far1"), load_list(far3, "far2")]
-        far_gates = far_gates + load_gates(gate2[D - 1 :], "last_far_gate")
+        near = [load_list(pos1, "near0")]
+        near_gates = load_gates(gate, "near_gates")
+        far.append(load_list(far2, "far1"))
+        near.append(load_list(pos2, "near1"))
+        far_gates = keep.tile([P, D * HALVES], F32, name="far_gates")
+        gate_runs = gate2.rearrange("d p (u v) -> (d p u) v", u=HALVES)
+        with nc.allow_non_contiguous_dma(reason="one gate value a partition"):
+            nc.sync.dma_start(far_gates[:], gate_runs[:: P + 1, :].rearrange("k v -> v k"))
+        near.append(load_list(pos3, "near2"))
+        far.append(load_list(far3, "far2"))
         cen_t = load_list(cen, "cen_t")
 
         ident = keep.tile([P, P], F32, name="ident")
         make_identity(nc, ident[:])
 
-        w_words = [load_words(words, "w_words%d" % i) for i, words in enumerate((w2_words, w3_words, w4_words))]
-        w_planes = []
-        for i, scales in enumerate((w2_scales, w3_scales, w4_scales)):
-            plane = keep.tile([P, N], U8, name="w_plane%d" % i, align_bytes=64)
-            nc.gpsimd.memset(plane[:].bitcast(I32), 0)
-            load_scale_rows(plane, scales)
-            w_planes.append(plane)
-
-        def quantize(values, name, pool=keep, tag=None):
+        def quantize(values, name):
             width = values.shape[1] // PACK
-            codes = pool.tile([P, width], U32, name=name + "_codes", tag=tag or name + "_codes", align_bytes=64)
-            plane = keep.tile([P, width], U8, name=name + "_plane", tag=name + "_plane", align_bytes=64)
+            codes = keep.tile([P, width], U32, name=name + "_codes", align_bytes=64)
+            plane = keep.tile([P, width], U8, name=name + "_plane", align_bytes=64)
             nc.vector.quantize_mx(out=codes[:].bitcast(FP8X4), scales=plane[:], in_=values)
             return codes[:], plane[:]
 
         halves = [slice(u * P, (u + 1) * P) for u in range(HALVES)]
-        node_halves = [slice(0, S // 2), slice(S // 2, S)]
         pieces = [slice(0, 256), slice(256, 384), slice(384, S)]
 
-        rounded_first = keep.tile([P, PACK, QUAD, PACK], BF16, name="rounded_first", align_bytes=64)
-        for rows in row_pairs:
-            nc.scalar.copy(rounded_first[:, :, :, rows].rearrange("p t q j -> p q j t"), w1_first[:, :, rows, :])
+        def rounded_tile(name, pairs_of_slots, pool=keep, offset=None):
+            shape = [P, pairs_of_slots, P // (PAIR * pairs_of_slots), PAIR, PACK]
+            return pool.tile(shape, BF16, name=name, align_bytes=64, offset=offset)
+
+        def walk_out(rounded):
+            return rounded.rearrange("p a q s j -> p q j a s")
+
+        def walk_in(raw):
+            return raw.rearrange("p j (q a s) -> p q j a s", a=PAIR, s=PAIR)
+
+        def flat_weights(rounded):
+            return rounded[:].rearrange("p a q s j -> p (a q s j)")
+
+        rounded_first = rounded_tile("rounded_first", PAIR)
+        for rows in row_parts:
+            nc.scalar.copy(walk_out(rounded_first[:, :, :, :, rows]), walk_in(first_raw[:, rows, :]))
 
         x_scale = keep.tile([P, S], U8, name="x_scale", align_bytes=64)
         nc.vector.tensor_copy(x_scale[:], x_plane[:].indirect(offs_t[:]))
-        first_q = quantize(rounded_first[:].rearrange("p t q j -> p (t q j)"), "w1_first", tag="chain")
+        first_q = quantize(flat_weights(rounded_first), "w1_first")
         x_codes = keep.tile([P, S], U32, name="x_codes", align_bytes=64)
         for cols in pieces:
             nc.vector.tensor_copy(x_codes[:, cols], x_table[:].bitcast(U32).indirect(offs_t[:, cols.start // 16 : cols.stop // 16]))
 
-        def product(acc, weights, cols):
-            nc.tensor.matmul_mx(
-                out=acc, lhsT=weights[0].bitcast(FP8X4), lhsT_scale=weights[1],
-                rhs=x_codes[:, cols].bitcast(FP8X4), rhs_scale=x_scale[:, cols],
-                start=True, stop=True,
-            )
-
-        def make_h(name, weights, parts, h_n=None):
-            if h_n is None:
-                h_n = keep.tile([P, S], F32, name=name)
-            for cols, bank, on_vector in parts:
+        def make_h(name, weights, parts, on_vector=False, pool=keep, offset=None):
+            h_n = pool.tile([P, S], F32, name=name, align_bytes=64, offset=offset)
+            for cols, bank in parts:
                 acc = banks.tile([P, cols.stop - cols.start], F32, name="%s_%d" % (name, cols.start), tag=bank)
-                product(acc[:], weights, cols)
+                nc.tensor.matmul_mx(
+                    out=acc[:], lhsT=weights[0].bitcast(FP8X4), lhsT_scale=weights[1],
+                    rhs=x_codes[:, cols].bitcast(FP8X4), rhs_scale=x_scale[:, cols],
+                    start=True, stop=True,
+                )
                 if on_vector:
                     nc.vector.tensor_relu(h_n[:, cols], acc[:])
                 else:
                     nc.scalar.activation(h_n[:, cols], acc[:], ACT.Relu)
             return h_n
 
-        h_first = make_h("h_first", first_q, [(pieces[0], "a", False), (pieces[1], "d", False), (pieces[2], "e", False)])
-        rounded_upper = keep.tile([P, PAIR, 2 * QUAD, PACK], BF16, name="rounded_upper", align_bytes=64)
-        nc.vector.tensor_copy(rounded_upper[:].rearrange("p s q j -> p q j s"), w1_upper[:, :, :, :PAIR])
-        rounded_mixed = keep.tile([P, PAIR, P, PACK], BF16, name="rounded_mixed", align_bytes=64)
-        nc.vector.tensor_copy(rounded_mixed[:, :, 2 * QUAD :, :].rearrange("p i q j -> p q j i"), w1_upper[:, :, :, PAIR:])
-        upper_q = quantize(rounded_upper[:].rearrange("p s q j -> p (s q j)"), "w1_upper")
-        codes = keep.tile([P, PAIR * P], U32, name="mixed_codes", align_bytes=64)
-        plane = keep.tile([P, PAIR * P], U8, name="mixed_plane", align_bytes=64)
+        whole = slice(0, S)
+        rounded_second = rounded_tile("rounded_second", PAIR, shared, 13 * H_BYTES + H_BYTES // 4)
+        nc.scalar.copy(walk_out(rounded_second[:]), walk_in(second_raw[:]))
+        h_first = make_h("h_first", first_q, list(zip(pieces, "pqr")), pool=shared, offset=14 * H_BYTES)
+        h_second = make_h("h_second", quantize(flat_weights(rounded_second), "w1_second"), [(whole, "d")], pool=shared, offset=17 * H_BYTES)
+        rounded_upper = [rounded_tile("rounded_upper%d" % a, 1, shared, 13 * H_BYTES + a * H_BYTES // 2) for a in range(PAIR)]
+        for a in range(PAIR):
+            nc.vector.tensor_copy(walk_out(rounded_upper[a][:]), walk_in(upper_raw[:])[:, :, :, a : a + 1, :])
+        upper_q = [quantize(flat_weights(rounded_upper[a]), "w1_upper%d" % a) for a in range(PAIR)]
 
-        def quantize_mixed(start):
-            for i in range(PAIR):
-                cols = slice(i * P + start, i * P + start + 2 * QUAD)
-                nc.vector.quantize_mx(
-                    out=codes[:, cols].bitcast(FP8X4), scales=plane[:, cols],
-                    in_=rounded_mixed[:, i, start : start + 2 * QUAD, :].rearrange("p m j -> p (m j)"),
-                )
 
-        quantize_mixed(2 * QUAD)
-        nc.scalar.copy(
-            rounded_mixed[:, :, : 2 * QUAD, :].rearrange("p i (a q) j -> p q j a i", a=2),
-            w1_second.rearrange("p q j (a i) -> p q j a i", a=2),
-        )
-        quantize_mixed(0)
-        h_upper = make_h(
-            "h_upper", upper_q, [(node_halves[0], "b", False), (node_halves[1], "e", False)],
-            shared.tile([P, S], F32, name="h_upper", offset=4096),
-        )
-        h_mixed = [
-            make_h("h_mixed%d" % i, (codes[:, halves[i]], plane[:, halves[i]]), [(slice(0, S), "ad"[i], False)]) for i in range(PAIR)
-        ]
-        own_low = keep.tile([P, S], F32, name="own_low")
-        own_high = [keep.tile([P, S], F32, name="own_high%d" % i) for i in range(PAIR)]
-        for s in range(PAIR):
-            nc.sync.dma_start(own_low[64 * s : 64 * s + 32, :], h_first[32 * s : 32 * s + 32, :])
-            nc.sync.dma_start(own_high[s][:32, :], h_first[64 + 32 * s : 96 + 32 * s, :])
-        for s in range(PAIR):
-            nc.sync.dma_start(own_low[64 * s + 32 : 64 * s + 64, :], h_mixed[s][:32, :])
-            nc.sync.dma_start(own_high[s][32:64, :], h_mixed[s][32:64, :])
-            nc.sync.dma_start(own_high[s][64:, :], h_mixed[s][64:, :])
+        own_windows = [shared.tile([P, S], F32, name="own_window%d" % t, align_bytes=64, offset=(1 + t) * H_BYTES) for t in range(PACK)]
 
-        def gather_sum(window, lists, gates, targets, opens, closes, split_last=False):
-            for d, held in enumerate(lists):
-                picked = ring.tile([P, V], F32, name="picked", align_bytes=64)[:]
-                if gates is None:
-                    nc.vector.tensor_copy(picked, window[:].indirect(held[:]))
-                elif split_last and d == D - 1:
-                    for cols in halves:
-                        part = window[:].indirect(held[:, cols.start // 16 : cols.stop // 16])
-                        nc.vector.tensor_tensor(picked[:, cols], part, gates[d][:, cols], MULT)
-                else:
-                    nc.vector.tensor_tensor(picked, window[:].indirect(held[:]), gates[d], MULT)
-                for u, cols in enumerate(halves):
-                    nc.tensor.matmul(
-                        targets[u], lhsT=picked[:, cols], rhs=ident[:], is_transpose=True,
-                        start=(d == 0 and u in opens), stop=(d == len(lists) - 1 and u in closes),
-                    )
+        def regroup(h_n, rows, slots):
+            count = rows.stop - rows.start
+            for i, a in enumerate(slots):
+                for s in range(PAIR):
+                    nc.sync.dma_start(own_windows[PAIR * a + s][rows, :], h_n[PAIR * count * i + s : PAIR * count * (i + 1) : PAIR, :])
 
         pairs = {
-            z: [shared.tile([P, PAIR, P, PAIR], BF16, name="pairs%d%d" % (z, u), offset=1024 * (HALVES * (z - 1) + u)) for u in range(HALVES)]
+            z: [shared.tile([P, PAIR, P, PAIR], BF16, name="pairs%d%d" % (z, u), align_bytes=64, offset=(6 + z) * H_BYTES + 4 * V * u) for u in range(HALVES)]
             for z in (1, 2)
         }
-        z_bf = [keep.tile([P, V, PACK], BF16, name="z_bf%d" % z, align_bytes=64) for z in range(3)]
+
+        def place(z, u, rows):
+            return pairs[z][u][:, :, rows, :].rearrange("v a q s -> v a (q s)")
+
+        def neighbours(tiles, columns, rows, near_banks, far_banks, after_list):
+            first_phase = len(near_banks) == 1
+            split_last = len(near_banks) > 1
+            if split_last:
+                sums = [banks.tile([P, PAIR, P], F32, name="near_sums%d" % u, tag=near_banks[u])[:] for u in range(HALVES)]
+                opens = closes = range(HALVES)
+            else:
+                held = banks.tile([P, HALVES, PAIR, P], F32, name="near_sums", tag=near_banks[0])
+                sums = [held[:, u, :, :] for u in range(HALVES)]
+                opens, closes = (0,), (HALVES - 1,)
+            running, all_turned = [], []
+
+            def add_far(d):
+                if d < D - 1 and first_phase:
+                    running.append(shared.tile([P, HALVES, PAIR, P], F32, name="lower_running", align_bytes=64, offset=16 * H_BYTES))
+                elif d < D - 1:
+                    running.append(ring.tile([P, HALVES, PAIR, P], F32, name="running", tag="running%d" % d))
+                for u in range(HALVES):
+                    weight = far_gates[:, HALVES * d + u : HALVES * d + u + 1]
+                    target = running[d][:, u, :, :] if d < D - 1 else place(2, u, rows)
+                    nc.vector.scalar_tensor_tensor(target, all_turned[d][:, u, :, :], weight, running[d - 1][:, u, :, :], MULT, ADD)
+
+            for d in range(D):
+                turned = banks.tile([P, HALVES, PAIR, P], F32, name="turned", tag=far_banks[d])
+                for i, h_n in enumerate(tiles):
+                    if split_last and d == D - 1 and i == 0:
+                        fetched = shared.tile([P, V], F32, name="late_fetched", align_bytes=64, offset=10 * H_BYTES)
+                    elif first_phase and d == D - 1 and i == 1:
+                        fetched = shared.tile([P, V], F32, name="third_fetched", align_bytes=64, offset=0)
+                    elif split_last and d == 0:
+                        fetched = shared.tile([P, V], F32, name="upper_fetched%d" % i, align_bytes=64, offset=15 * H_BYTES + 4 * V * i)
+                    else:
+                        fetched = ring.tile([P, V], F32, name="fetched", tag="far", align_bytes=64)
+                    nc.scalar.activation(fetched[:], h_n[:].indirect(far[d][:]), ACT.Copy)
+                    for u, cols in enumerate(halves):
+                        nc.tensor.transpose(columns(turned[:, u, :, :], i), fetched[:, cols], ident[:])
+                picked = [
+                    shared.tile([P, V], F32, name="early_picked%d%d" % (d, i), align_bytes=64, offset=11 * H_BYTES + 4 * V * (PAIR * d + i))
+                    if first_phase and d < PAIR
+                    else shared.tile([P, V], F32, name="late_picked", align_bytes=64, offset=16 * H_BYTES) if first_phase and i == 0
+                    else ring.tile([P, V], F32, name="picked", tag="near", align_bytes=64)
+                    for i in range(PAIR)
+                ]
+                if split_last and d == D - 1:
+                    steps = [(i, [u]) for u in range(HALVES) for i in range(PAIR)]
+                else:
+                    steps = [(i, range(HALVES)) for i in range(PAIR)]
+                for i, us in steps:
+                    cols = slice(halves[us[0]].start, halves[us[-1]].stop)
+                    part = tiles[i][:].indirect(near[d][:, cols.start // 16 : cols.stop // 16])
+                    nc.vector.tensor_tensor(picked[i][:, cols], part, near_gates[d][:, cols], MULT)
+                    for u in us:
+                        nc.tensor.matmul(
+                            columns(sums[u], i), lhsT=picked[i][:, halves[u]], rhs=ident[:], is_transpose=True,
+                            start=(d == 0 and i == 0 and u in opens), stop=(d == D - 1 and i == PAIR - 1 and u in closes),
+                        )
+                all_turned.append(turned)
+                if d == 0:
+                    running.append(ring.tile([P, HALVES, PAIR, P], F32, name="running", tag="running0"))
+                    for u in range(HALVES):
+                        nc.scalar.activation(running[0][:, u, :, :], turned[:, u, :, :], ACT.Copy, scale=far_gates[:, u : u + 1])
+                after_list(d)
+                if split_last and d == 1:
+                    add_far(d)
+
+            return sums, add_far
+
+        def quarter_columns(region, i):
+            return region[:, :, 2 * QUAD * i : 2 * QUAD * (i + 1)]
+
+        def slot_columns(region, i):
+            return region[:, i, :]
 
         def words_of(values):
-            return values.rearrange("p v t -> p (v t)").bitcast(F32).rearrange("p (v a) -> p v a", a=PACK // PAIR)
+            return values.rearrange("p v t -> p (v t)").bitcast(F32).rearrange("p (v a) -> p v a", a=PAIR)
 
-        def turn_back(target, values):
-            nc.tensor.transpose(target, values.rearrange("v p s -> v (p s)").bitcast(F32), ident[:])
-
-        def round_upper(z, u, acc):
-            nc.scalar.copy(pairs[z][u][:, 0, 2 * QUAD :, :], acc.rearrange("v (s q) -> v q s", s=PAIR))
-
-        def round_mixed(z, acc):
-            for u in range(HALVES):
-                nc.scalar.copy(pairs[z][u][:, 1, QUAD:, :], acc[:, u, :, QUAD:].rearrange("v i m -> v m i"))
-                nc.scalar.copy(pairs[z][u][:, 0, QUAD : 2 * QUAD, :], acc[:, u, :, :QUAD].rearrange("v i m -> v m i"))
-
-        sets = {1: (near, first_gate + later_gates), 2: (far, far_gates)}
-
-        acc = banks.tile([P, 2, HALVES, P], F32, name="first_sums", tag="x")
-        gather_sum(h_first, *sets[1], [acc[:, 0, u, :] for u in range(HALVES)], (0,), ())
-        gather_sum(h_first, *sets[2], [acc[:, 1, u, :] for u in range(HALVES)], (), (1,))
-        for z in (1, 2):
-            for u in range(HALVES):
-                nc.scalar.copy(pairs[z][u][:, :, :QUAD, :], acc[:, z - 1, u, :].rearrange("v (a s q) -> v a q s", a=2, s=PAIR))
-
-        acc = banks.tile([P, HALVES, P], F32, name="upper_near", tag="y")
-        gather_sum(h_upper, *sets[1], [acc[:, u, :] for u in range(HALVES)], (0,), (1,))
-        for u in range(HALVES):
-            round_upper(1, u, acc[:, u, :])
-        own_acc = banks.tile([P, HALVES, PAIR, P], F32, name="own_acc", tag="e")
-        gather_sum(h_upper, [cen_t], None, [own_acc[:, u, 1, :] for u in range(HALVES)], (0,), ())
-
-        acc = banks.tile([P, HALVES, PAIR, P], F32, name="mixed_near", tag="z")
-        for i in range(PAIR):
-            gather_sum(h_mixed[i], *sets[1], [acc[:, u, i, :] for u in range(HALVES)], (0,) if i == 0 else (), (1,) if i == 1 else ())
-        round_mixed(1, acc)
-        back = banks.tile([P, HALVES, PAIR, P], F32, name="near_back", tag="b")
-        for u in range(HALVES):
+        def turn_back(target, z, u):
             for a in range(PAIR):
-                turn_back(back[:, u, a, :], pairs[1][u][:, a, :, :])
-        nc.scalar.copy(words_of(z_bf[1][:]).rearrange("p (u v) a -> p u v a", u=HALVES), back[:].rearrange("p u a v -> p u v a"))
+                nc.tensor.transpose(target[:, a, :], pairs[z][u][:, a, :, :].rearrange("v p s -> v (p s)").bitcast(F32), ident[:])
 
-        acc = banks.tile([P, HALVES, PAIR, P], F32, name="mixed_far", tag="x")
-        gather_sum(h_mixed[0], *sets[2], [acc[:, u, 0, :] for u in range(HALVES)], (0,), ())
-        gather_sum(own_low, [cen_t], None, [own_acc[:, u, 0, :] for u in range(HALVES)], (), (1,))
-        own_pairs = keep.tile([P, HALVES, P, PAIR], BF16, name="own_pairs")
-        nc.scalar.copy(own_pairs[:].rearrange("v u (i q) s -> v u i q s", i=PAIR), own_acc[:].rearrange("v u i (s q) -> v u i q s", s=PAIR))
-        own_back = banks.tile([P, V], F32, name="own_back", tag="y")
-        for u, cols in enumerate(halves):
-            turn_back(own_back[:, cols], own_pairs[:, u, :, :])
-        nc.scalar.copy(words_of(z_bf[0][:])[:, :, 0], own_back[:])
+        both = range(PAIR)
+        lower_rows, upper_rows = slice(0, 2 * QUAD), slice(2 * QUAD, P)
+        regroup(h_first, slice(0, QUAD), both)
+        regroup(h_second, slice(QUAD, 2 * QUAD), both)
+        h_upper = []
 
-        gather_sum(h_mixed[1], *sets[2], [acc[:, u, 1, :] for u in range(HALVES)], (), (1,))
-        round_mixed(2, acc)
-        far_back = [banks.tile([P, PAIR, P], F32, name="far_back%d" % u, tag="cd"[u]) for u in range(HALVES)]
+        def make_upper(d):
+            for a in range(PAIR if d == D - 1 else 0):
+                h_upper.append(make_h("h_upper%d" % a, upper_q[a], [(whole, "bc"[a])], on_vector=a == 1, pool=shared, offset=(14, 17)[a] * H_BYTES))
+
+        sums, add_lower = neighbours([h_first, h_second], quarter_columns, lower_rows, "x", "pqr", make_upper)
+        add_lower(1)
         for u in range(HALVES):
-            turn_back(far_back[u][:, 1, :], pairs[2][u][:, 1, :, :])
+            nc.vector.tensor_copy(place(1, u, lower_rows), sums[u])
+        for a in range(PAIR):
+            regroup(h_upper[a], upper_rows, range(a, a + 1))
 
-        accs = [banks.tile([P, P], F32, name="upper_far%d" % u, tag="za"[u]) for u in range(HALVES)]
-        gather_sum(h_upper, *sets[2], [held[:] for held in accs], (0, 1), (0, 1), split_last=True)
+        def finish_lower(d):
+            if d == 1:
+                add_lower(D - 1)
+
+        sums, add_upper = neighbours(h_upper, slot_columns, upper_rows, "yb", "dpq", finish_lower)
+        add_upper(D - 1)
+        w_words = [load_words(words, "w_words%d" % i, shared, 15 * H_BYTES + 4 * N * i) for i, words in enumerate((w2_words, w3_words, w4_words))]
+        staged_rows = shared.tile([16, 3 * N], U8, name="staged_rows", align_bytes=64, offset=0)
+        for i, scales in enumerate((w2_scales, w3_scales, w4_scales)):
+            nc.sync.dma_start(staged_rows[:, N * i : N * (i + 1)].bitcast(I32), scales[0].bitcast(I32))
+        all_planes = keep.tile([P, 3 * N], U8, name="all_planes", align_bytes=64)
+        nc.gpsimd.memset(all_planes[:].bitcast(I32), 0)
+        for q in range(4):
+            nc.sync.dma_start(all_planes[32 * q : 32 * q + 4, :].bitcast(I32), staged_rows[4 * q : 4 * q + 4, :].bitcast(I32))
+        w_planes = [all_planes[:, N * i : N * (i + 1)] for i in range(3)]
+
+        own = shared.tile([P, PACK, V], BF16, name="own", align_bytes=64, offset=10 * H_BYTES)
+        for t in range(PACK):
+            nc.scalar.activation(own[:, t, :], own_windows[t][:].indirect(cen_t[:]), ACT.Copy)
+        z_bf = [shared.tile([P, V, PACK], BF16, name="z_bf%d" % z, align_bytes=64, offset=at * H_BYTES // 2) for z, at in enumerate((14, 7, 9))]
+        far_back = banks.tile([P, HALVES, PAIR, P], F32, name="far_back", tag="r")
         for u in range(HALVES):
-            round_upper(2, u, accs[u][:])
-            turn_back(far_back[u][:, 0, :], pairs[2][u][:, 0, :, :])
+            turn_back(far_back[:, u, :, :], 2, u)
+        nc.scalar.copy(words_of(z_bf[2][:]).rearrange("p (u v) a -> p u v a", u=HALVES), far_back[:].rearrange("p u a v -> p u v a"))
         for u, cols in enumerate(halves):
-            nc.scalar.copy(words_of(z_bf[2][:, cols, :]), far_back[u][:].rearrange("p a v -> p v a"))
-        own = ring.tile([P, PAIR, V], BF16, name="own", tag="picked", align_bytes=64)
-        for s in range(PAIR):
-            nc.vector.tensor_copy(own[:, s, :], own_high[s][:].indirect(cen_t[:]))
-        z1_codes = ring.tile([P, V], U32, name="z1_codes", tag="picked", align_bytes=64)
-        z1_plane = keep.tile([P, V], U8, name="z1_plane", align_bytes=64)
+            nc.vector.tensor_copy(place(1, u, upper_rows), sums[u])
+            near_back = banks.tile([P, PAIR, P], F32, name="near_back%d" % u, tag="xc"[u])
+            turn_back(near_back[:], 1, u)
+            nc.scalar.copy(words_of(z_bf[1][:, cols, :]), near_back[:].rearrange("p a v -> p v a"))
 
         def flat(z, cols):
             return z_bf[z][:, cols, :].rearrange("p v t -> p (v t)")
 
-        def quantize_z1(cols):
-            nc.vector.quantize_mx(out=z1_codes[:, cols].bitcast(FP8X4), scales=z1_plane[:, cols], in_=flat(1, cols))
-
-        quantize_z1(halves[0])
-        nc.vector.tensor_copy(z_bf[0][:, :, PAIR:], own[:].rearrange("p s v -> p v s"))
-        quantize_z1(halves[1])
-
-        def last_pass(result, i, codes, plane, start, stop):
+        def last_pass(result, z, codes, plane, start, stop):
             nc.tensor.matmul_mx(
-                out=result[:], lhsT=w_words[i][:].bitcast(FP8X4), lhsT_scale=w_planes[i][:],
+                out=result[:], lhsT=w_words[z][:].bitcast(FP8X4), lhsT_scale=w_planes[z],
                 rhs=codes.bitcast(FP8X4), rhs_scale=plane, start=start, stop=stop,
             )
 
-        results = [banks.tile([P, P], F32, name="result%d" % u, tag="ac"[u]) for u in range(HALVES)]
+        results = [banks.tile([P, P], F32, name="result%d" % u, tag="dp"[u]) for u in range(HALVES)]
+        for cols in halves:
+            nc.vector.tensor_copy(z_bf[0][:, cols, :], own[:, :, cols].rearrange("p t v -> p v t"))
+        for z in (0, 2):
+            for u, cols in enumerate(halves):
+                last_pass(results[u], z, *quantize(flat(z, cols), "z%d_%d" % (z, u)), z == 0, False)
         for u, cols in enumerate(halves):
-            last_pass(results[u], 1, z1_codes[:, cols], z1_plane[:, cols], True, False)
-            codes, plane = quantize(flat(0, cols), "z0_%d" % u)
-            last_pass(results[u], 0, codes, plane, False, False)
-        for u, cols in enumerate(halves):
-            codes, plane = quantize(flat(2, cols), "z2_%d" % u)
-            last_pass(results[u], 2, codes, plane, False, True)
+            last_pass(results[u], 1, *quantize(flat(1, cols), "z1_%d" % u), False, True)
             staged = keep.tile([P, P], F32, name="staged%d" % u)
             nc.scalar.activation(staged[:], results[u][:], ACT.Tanh)
             nc.sync.dma_start(out[:, cols], staged[:])

@@ -54,32 +54,31 @@ def tile_picked_zmix_tanh_p_kernel(
 
         w1_rows = w1.rearrange("(p j) c -> p j c", j=PACK)
 
-        row_parts = [slice(0, 1), slice(1, PACK)]
-        first_raw = keep.tile([P, PACK, P], F32, name="first_raw")
-        nc.sync.dma_start(first_raw[:, row_parts[0], :], w1_rows[:, row_parts[0], :P])
         offs_t = load_list(offs, "offs_t")
         x_plane = keep.tile([P, T], U8, name="x_plane", align_bytes=64)
         for q in range(4):
             rows = x_scales[0, 4 * q : 4 * q + 4, :].bitcast(I32)
             (nc.sync, nc.scalar)[q % 2].dma_start(x_plane[32 * q : 32 * q + 32, :].bitcast(I32), rows.unsqueeze(0).to_broadcast([8, 4, T // 4]))
-        nc.sync.dma_start(first_raw[:, row_parts[1], :], w1_rows[:, row_parts[1], :P])
         x_table = load_words(x_words, "x_table")
+        first_raw = keep.tile([P, PACK, P], F32, name="first_raw")
+        nc.sync.dma_start(first_raw[:], w1_rows[:, :, :P])
         second_raw = shared.tile([P, PACK, P], F32, name="second_raw", align_bytes=64, offset=14 * H_BYTES)
         nc.sync.dma_start(second_raw[:], w1_rows[:, :, P : 2 * P])
         upper_raw = shared.tile([P, PACK, 2 * P], F32, name="upper_raw", align_bytes=64, offset=11 * H_BYTES)
         nc.sync.dma_start(upper_raw[:], w1_rows[:, :, 2 * P :])
         far = [load_list(far1, "far0")]
+        near_gates = load_gates(gate[:1], "first_gate")
         near = [load_list(pos1, "near0")]
-        near_gates = load_gates(gate, "near_gates")
         far.append(load_list(far2, "far1"))
         near.append(load_list(pos2, "near1"))
+        near_gates = near_gates + load_gates(gate[1:], "later_gates")
+        near.append(load_list(pos3, "near2"))
+        far.append(load_list(far3, "far2"))
+        cen_t = load_list(cen, "cen_t")
         far_gates = keep.tile([P, D * HALVES], F32, name="far_gates")
         gate_runs = gate2.rearrange("d p (u v) -> (d p u) v", u=HALVES)
         with nc.allow_non_contiguous_dma(reason="one gate value a partition"):
             nc.sync.dma_start(far_gates[:], gate_runs[:: P + 1, :].rearrange("k v -> v k"))
-        near.append(load_list(pos3, "near2"))
-        far.append(load_list(far3, "far2"))
-        cen_t = load_list(cen, "cen_t")
 
         ident = keep.tile([P, P], F32, name="ident")
         make_identity(nc, ident[:])
@@ -108,8 +107,7 @@ def tile_picked_zmix_tanh_p_kernel(
             return rounded[:].rearrange("p a q s j -> p (a q s j)")
 
         rounded_first = rounded_tile("rounded_first", PAIR)
-        for rows in row_parts:
-            nc.scalar.copy(walk_out(rounded_first[:, :, :, :, rows]), walk_in(first_raw[:, rows, :]))
+        nc.scalar.copy(walk_out(rounded_first[:]), walk_in(first_raw[:]))
 
         x_scale = keep.tile([P, S], U8, name="x_scale", align_bytes=64)
         nc.vector.tensor_copy(x_scale[:], x_plane[:].indirect(offs_t[:]))
@@ -144,13 +142,17 @@ def tile_picked_zmix_tanh_p_kernel(
         upper_q = [quantize(flat_weights(rounded_upper[a]), "w1_upper%d" % a) for a in range(PAIR)]
 
 
-        own_windows = [shared.tile([P, S], F32, name="own_window%d" % t, align_bytes=64, offset=(1 + t) * H_BYTES) for t in range(PACK)]
+        own = keep.tile([P, PACK, V], BF16, name="own")
 
-        def regroup(h_n, rows, slots):
-            count = rows.stop - rows.start
+        def fetch_own(h_n, rows, slots, on_vector=False):
+            values = ring.tile([P, V], BF16, name="own_values", tag="own")
+            if on_vector:
+                nc.vector.tensor_copy(values[:], h_n[:].indirect(cen_t[:]))
+            else:
+                nc.scalar.activation(values[:], h_n[:].indirect(cen_t[:]), ACT.Copy)
+            count = PAIR * (rows.stop - rows.start)
             for i, a in enumerate(slots):
-                for s in range(PAIR):
-                    nc.sync.dma_start(own_windows[PAIR * a + s][rows, :], h_n[PAIR * count * i + s : PAIR * count * (i + 1) : PAIR, :])
+                nc.sync.dma_start(own[rows, PAIR * a : PAIR * (a + 1), :], values[count * i : count * (i + 1), :])
 
         pairs = {
             z: [shared.tile([P, PAIR, P, PAIR], BF16, name="pairs%d%d" % (z, u), align_bytes=64, offset=(6 + z) * H_BYTES + 4 * V * u) for u in range(HALVES)]
@@ -185,9 +187,7 @@ def tile_picked_zmix_tanh_p_kernel(
             for d in range(D):
                 turned = banks.tile([P, HALVES, PAIR, P], F32, name="turned", tag=far_banks[d])
                 for i, h_n in enumerate(tiles):
-                    if split_last and d == D - 1 and i == 0:
-                        fetched = shared.tile([P, V], F32, name="late_fetched", align_bytes=64, offset=10 * H_BYTES)
-                    elif first_phase and d == D - 1 and i == 1:
+                    if first_phase and d == D - 1 and i == 1:
                         fetched = shared.tile([P, V], F32, name="third_fetched", align_bytes=64, offset=0)
                     elif split_last and d == 0:
                         fetched = shared.tile([P, V], F32, name="upper_fetched%d" % i, align_bytes=64, offset=15 * H_BYTES + 4 * V * i)
@@ -200,6 +200,7 @@ def tile_picked_zmix_tanh_p_kernel(
                     shared.tile([P, V], F32, name="early_picked%d%d" % (d, i), align_bytes=64, offset=11 * H_BYTES + 4 * V * (PAIR * d + i))
                     if first_phase and d < PAIR
                     else shared.tile([P, V], F32, name="late_picked", align_bytes=64, offset=16 * H_BYTES) if first_phase and i == 0
+                    else shared.tile([P, V], F32, name="last_picked%d" % i, align_bytes=64, offset=H_BYTES + 4 * V * i) if split_last and d == D - 1
                     else ring.tile([P, V], F32, name="picked", tag="near", align_bytes=64)
                     for i in range(PAIR)
                 ]
@@ -242,11 +243,12 @@ def tile_picked_zmix_tanh_p_kernel(
 
         both = range(PAIR)
         lower_rows, upper_rows = slice(0, 2 * QUAD), slice(2 * QUAD, P)
-        regroup(h_first, slice(0, QUAD), both)
-        regroup(h_second, slice(QUAD, 2 * QUAD), both)
         h_upper = []
 
         def make_upper(d):
+            if d == D - 1:
+                fetch_own(h_first, slice(0, QUAD), both, on_vector=True)
+                fetch_own(h_second, slice(QUAD, 2 * QUAD), both)
             for a in range(PAIR if d == D - 1 else 0):
                 h_upper.append(make_h("h_upper%d" % a, upper_q[a], [(whole, "bc"[a])], on_vector=a == 1, pool=shared, offset=(14, 17)[a] * H_BYTES))
 
@@ -254,15 +256,14 @@ def tile_picked_zmix_tanh_p_kernel(
         add_lower(1)
         for u in range(HALVES):
             nc.vector.tensor_copy(place(1, u, lower_rows), sums[u])
-        for a in range(PAIR):
-            regroup(h_upper[a], upper_rows, range(a, a + 1))
 
         def finish_lower(d):
+            for a in range(PAIR if d == 0 else 0):
+                fetch_own(h_upper[a], upper_rows, range(a, a + 1))
             if d == 1:
                 add_lower(D - 1)
 
         sums, add_upper = neighbours(h_upper, slot_columns, upper_rows, "yb", "dpq", finish_lower)
-        add_upper(D - 1)
         w_words = [load_words(words, "w_words%d" % i, shared, 15 * H_BYTES + 4 * N * i) for i, words in enumerate((w2_words, w3_words, w4_words))]
         staged_rows = shared.tile([16, 3 * N], U8, name="staged_rows", align_bytes=64, offset=0)
         for i, scales in enumerate((w2_scales, w3_scales, w4_scales)):
@@ -273,19 +274,17 @@ def tile_picked_zmix_tanh_p_kernel(
             nc.sync.dma_start(all_planes[32 * q : 32 * q + 4, :].bitcast(I32), staged_rows[4 * q : 4 * q + 4, :].bitcast(I32))
         w_planes = [all_planes[:, N * i : N * (i + 1)] for i in range(3)]
 
-        own = shared.tile([P, PACK, V], BF16, name="own", align_bytes=64, offset=10 * H_BYTES)
-        for t in range(PACK):
-            nc.scalar.activation(own[:, t, :], own_windows[t][:].indirect(cen_t[:]), ACT.Copy)
-        z_bf = [shared.tile([P, V, PACK], BF16, name="z_bf%d" % z, align_bytes=64, offset=at * H_BYTES // 2) for z, at in enumerate((14, 7, 9))]
-        far_back = banks.tile([P, HALVES, PAIR, P], F32, name="far_back", tag="r")
-        for u in range(HALVES):
-            turn_back(far_back[:, u, :, :], 2, u)
-        nc.scalar.copy(words_of(z_bf[2][:]).rearrange("p (u v) a -> p u v a", u=HALVES), far_back[:].rearrange("p u a v -> p u v a"))
+        z_bf = [shared.tile([P, V, PACK], BF16, name="z_bf%d" % z, align_bytes=64, offset=(1 + z) * H_BYTES) for z in range(3)]
         for u, cols in enumerate(halves):
-            nc.vector.tensor_copy(place(1, u, upper_rows), sums[u])
+            nc.scalar.copy(place(1, u, upper_rows), sums[u])
             near_back = banks.tile([P, PAIR, P], F32, name="near_back%d" % u, tag="xc"[u])
             turn_back(near_back[:], 1, u)
             nc.scalar.copy(words_of(z_bf[1][:, cols, :]), near_back[:].rearrange("p a v -> p v a"))
+        add_upper(D - 1)
+        for u, cols in enumerate(halves):
+            far_back = banks.tile([P, PAIR, P], F32, name="far_back%d" % u, tag="ry"[u])
+            turn_back(far_back[:], 2, u)
+            nc.scalar.copy(words_of(z_bf[2][:, cols, :]), far_back[:].rearrange("p a v -> p v a"))
 
         def flat(z, cols):
             return z_bf[z][:, cols, :].rearrange("p v t -> p (v t)")
@@ -299,11 +298,11 @@ def tile_picked_zmix_tanh_p_kernel(
         results = [banks.tile([P, P], F32, name="result%d" % u, tag="dp"[u]) for u in range(HALVES)]
         for cols in halves:
             nc.vector.tensor_copy(z_bf[0][:, cols, :], own[:, :, cols].rearrange("p t v -> p v t"))
-        for z in (0, 2):
+        for z in range(2):
             for u, cols in enumerate(halves):
                 last_pass(results[u], z, *quantize(flat(z, cols), "z%d_%d" % (z, u)), z == 0, False)
         for u, cols in enumerate(halves):
-            last_pass(results[u], 1, *quantize(flat(1, cols), "z1_%d" % u), False, True)
+            last_pass(results[u], 2, *quantize(flat(2, cols), "z2_%d" % u), False, True)
             staged = keep.tile([P, P], F32, name="staged%d" % u)
             nc.scalar.activation(staged[:], results[u][:], ACT.Tanh)
             nc.sync.dma_start(out[:, cols], staged[:])

@@ -69,29 +69,26 @@ def tile_picked_zmix_tanh_p_kernel(
         far = [load_list(far1, "far0")]
         near_gates = load_gates(gate[:1], "first_gate")
         near = [load_list(pos1, "near0")]
-        far.append(load_list(far2, "far1"))
         near.append(load_list(pos2, "near1"))
         near_gates = near_gates + load_gates(gate[1:], "later_gates")
         near.append(load_list(pos3, "near2"))
-        far.append(load_list(far3, "far2"))
         cen_t = load_list(cen, "cen_t")
-        far_gates = keep.tile([P, D * HALVES], F32, name="far_gates")
-        gate_runs = gate2.rearrange("d p (u v) -> (d p u) v", u=HALVES)
-        with nc.allow_non_contiguous_dma(reason="one gate value a partition"):
-            nc.sync.dma_start(far_gates[:], gate_runs[:: P + 1, :].rearrange("k v -> v k"))
+        far.append(load_list(far2, "far1"))
+        far.append(load_list(far3, "far2"))
+        wide_gates = load_gates(gate2, "wide_gates")
 
         ident = keep.tile([P, P], F32, name="ident")
         make_identity(nc, ident[:])
 
-        def quantize(values, name):
+        def quantize(values, name, pool=keep, offset=None):
             width = values.shape[1] // PACK
-            codes = keep.tile([P, width], U32, name=name + "_codes", align_bytes=64)
+            codes = pool.tile([P, width], U32, name=name + "_codes", align_bytes=64, offset=offset)
             plane = keep.tile([P, width], U8, name=name + "_plane", align_bytes=64)
             nc.vector.quantize_mx(out=codes[:].bitcast(FP8X4), scales=plane[:], in_=values)
             return codes[:], plane[:]
 
         halves = [slice(u * P, (u + 1) * P) for u in range(HALVES)]
-        pieces = [slice(0, 256), slice(256, 384), slice(384, S)]
+        pieces = [slice(0, 256), slice(256, S)]
 
         def rounded_tile(name, pairs_of_slots, pool=keep, offset=None):
             shape = [P, pairs_of_slots, P // (PAIR * pairs_of_slots), PAIR, PACK]
@@ -116,8 +113,8 @@ def tile_picked_zmix_tanh_p_kernel(
         for cols in pieces:
             nc.vector.tensor_copy(x_codes[:, cols], x_table[:].bitcast(U32).indirect(offs_t[:, cols.start // 16 : cols.stop // 16]))
 
-        def make_h(name, weights, parts, on_vector=False, pool=keep, offset=None):
-            h_n = pool.tile([P, S], F32, name=name, align_bytes=64, offset=offset)
+        def multiply(name, weights, parts):
+            products = []
             for cols, bank in parts:
                 acc = banks.tile([P, cols.stop - cols.start], F32, name="%s_%d" % (name, cols.start), tag=bank)
                 nc.tensor.matmul_mx(
@@ -125,21 +122,25 @@ def tile_picked_zmix_tanh_p_kernel(
                     rhs=x_codes[:, cols].bitcast(FP8X4), rhs_scale=x_scale[:, cols],
                     start=True, stop=True,
                 )
-                if on_vector:
-                    nc.vector.tensor_relu(h_n[:, cols], acc[:])
-                else:
-                    nc.scalar.activation(h_n[:, cols], acc[:], ACT.Relu)
+                products.append((cols, acc))
+            return products
+
+        def make_h(name, products, pool=keep, offset=None):
+            h_n = pool.tile([P, S], F32, name=name, align_bytes=64, offset=offset)
+            for cols, acc in products:
+                nc.scalar.activation(h_n[:, cols], acc[:], ACT.Relu)
             return h_n
 
         whole = slice(0, S)
         rounded_second = rounded_tile("rounded_second", PAIR, shared, 13 * H_BYTES + H_BYTES // 4)
         nc.scalar.copy(walk_out(rounded_second[:]), walk_in(second_raw[:]))
-        h_first = make_h("h_first", first_q, list(zip(pieces, "pqr")), pool=shared, offset=14 * H_BYTES)
-        h_second = make_h("h_second", quantize(flat_weights(rounded_second), "w1_second"), [(whole, "d")], pool=shared, offset=17 * H_BYTES)
+        h_first = make_h("h_first", multiply("first", first_q, list(zip(pieces, "pq"))), shared, 14 * H_BYTES)
+        h_second = make_h("h_second", multiply("second", quantize(flat_weights(rounded_second), "w1_second"), [(whole, "d")]))
         rounded_upper = [rounded_tile("rounded_upper%d" % a, 1, shared, 13 * H_BYTES + a * H_BYTES // 2) for a in range(PAIR)]
         for a in range(PAIR):
             nc.vector.tensor_copy(walk_out(rounded_upper[a][:]), walk_in(upper_raw[:])[:, :, :, a : a + 1, :])
         upper_q = [quantize(flat_weights(rounded_upper[a]), "w1_upper%d" % a) for a in range(PAIR)]
+        upper_products = [multiply("upper%d" % a, upper_q[a], [(whole, "bc"[a])]) for a in range(PAIR)]
 
 
         own = keep.tile([P, PACK, V], BF16, name="own")
@@ -154,79 +155,70 @@ def tile_picked_zmix_tanh_p_kernel(
             for i, a in enumerate(slots):
                 nc.sync.dma_start(own[rows, PAIR * a : PAIR * (a + 1), :], values[count * i : count * (i + 1), :])
 
+        near_pairs = keep.tile([P, HALVES, PAIR, P, PAIR], BF16, name="near_pairs", align_bytes=64)
         pairs = {
-            z: [shared.tile([P, PAIR, P, PAIR], BF16, name="pairs%d%d" % (z, u), align_bytes=64, offset=(6 + z) * H_BYTES + 4 * V * u) for u in range(HALVES)]
-            for z in (1, 2)
+            1: [near_pairs[:, u, :, :, :] for u in range(HALVES)],
+            2: [keep.tile([P, PAIR, P, PAIR], BF16, name="far_pairs%d" % u, align_bytes=64)[:] for u in range(HALVES)],
         }
+
+        def place_near(rows):
+            return near_pairs[:, :, :, rows, :].rearrange("v u a q s -> v u a (q s)")
 
         def place(z, u, rows):
             return pairs[z][u][:, :, rows, :].rearrange("v a q s -> v a (q s)")
 
-        def neighbours(tiles, columns, rows, near_banks, far_banks, after_list):
-            first_phase = len(near_banks) == 1
-            split_last = len(near_banks) > 1
-            if split_last:
-                sums = [banks.tile([P, PAIR, P], F32, name="near_sums%d" % u, tag=near_banks[u])[:] for u in range(HALVES)]
-                opens = closes = range(HALVES)
-            else:
-                held = banks.tile([P, HALVES, PAIR, P], F32, name="near_sums", tag=near_banks[0])
-                sums = [held[:, u, :, :] for u in range(HALVES)]
-                opens, closes = (0,), (HALVES - 1,)
-            running, all_turned = [], []
+        def spot(name, shape, dtype, offset):
+            return shared.tile(shape, dtype, name=name, align_bytes=64, offset=offset)
 
-            def add_far(d):
-                if d < D - 1 and first_phase:
-                    running.append(shared.tile([P, HALVES, PAIR, P], F32, name="lower_running", align_bytes=64, offset=16 * H_BYTES))
-                elif d < D - 1:
-                    running.append(ring.tile([P, HALVES, PAIR, P], F32, name="running", tag="running%d" % d))
-                for u in range(HALVES):
-                    weight = far_gates[:, HALVES * d + u : HALVES * d + u + 1]
-                    target = running[d][:, u, :, :] if d < D - 1 else place(2, u, rows)
-                    nc.vector.scalar_tensor_tensor(target, all_turned[d][:, u, :, :], weight, running[d - 1][:, u, :, :], MULT, ADD)
+        def phase(tiles, columns, rows, sums):
+            turned, running = {}, {}
 
-            for d in range(D):
-                turned = banks.tile([P, HALVES, PAIR, P], F32, name="turned", tag=far_banks[d])
+            def far_list(d, bank, spots={}):
+                held = banks.tile([P, HALVES, PAIR, P], F32, name="turned", tag=bank)
+                turned[d] = [held[:, u, :, :] for u in range(HALVES)]
                 for i, h_n in enumerate(tiles):
-                    if first_phase and d == D - 1 and i == 1:
-                        fetched = shared.tile([P, V], F32, name="third_fetched", align_bytes=64, offset=0)
-                    elif split_last and d == 0:
-                        fetched = shared.tile([P, V], F32, name="upper_fetched%d" % i, align_bytes=64, offset=15 * H_BYTES + 4 * V * i)
+                    if i in spots:
+                        fetched = spot("held_fetched", [P, V], F32, spots[i])
                     else:
                         fetched = ring.tile([P, V], F32, name="fetched", tag="far", align_bytes=64)
                     nc.scalar.activation(fetched[:], h_n[:].indirect(far[d][:]), ACT.Copy)
                     for u, cols in enumerate(halves):
-                        nc.tensor.transpose(columns(turned[:, u, :, :], i), fetched[:, cols], ident[:])
+                        nc.tensor.transpose(columns(turned[d][u], i), fetched[:, cols], ident[:])
+
+            def near_list(d, spots={}, by_halves=False, lists=near, gates=near_gates, sums=sums):
                 picked = [
-                    shared.tile([P, V], F32, name="early_picked%d%d" % (d, i), align_bytes=64, offset=11 * H_BYTES + 4 * V * (PAIR * d + i))
-                    if first_phase and d < PAIR
-                    else shared.tile([P, V], F32, name="late_picked", align_bytes=64, offset=16 * H_BYTES) if first_phase and i == 0
-                    else shared.tile([P, V], F32, name="last_picked%d" % i, align_bytes=64, offset=H_BYTES + 4 * V * i) if split_last and d == D - 1
-                    else ring.tile([P, V], F32, name="picked", tag="near", align_bytes=64)
+                    spot("held_picked", [P, V], F32, spots[i]) if i in spots else ring.tile([P, V], F32, name="picked", tag="near", align_bytes=64)
                     for i in range(PAIR)
                 ]
-                if split_last and d == D - 1:
+                if by_halves:
                     steps = [(i, [u]) for u in range(HALVES) for i in range(PAIR)]
                 else:
                     steps = [(i, range(HALVES)) for i in range(PAIR)]
                 for i, us in steps:
                     cols = slice(halves[us[0]].start, halves[us[-1]].stop)
-                    part = tiles[i][:].indirect(near[d][:, cols.start // 16 : cols.stop // 16])
-                    nc.vector.tensor_tensor(picked[i][:, cols], part, near_gates[d][:, cols], MULT)
+                    part = tiles[i][:].indirect(lists[d][:, cols.start // 16 : cols.stop // 16])
+                    nc.vector.tensor_tensor(picked[i][:, cols], part, gates[d][:, cols], MULT)
                     for u in us:
+                        region, opens, closes = sums[u]
                         nc.tensor.matmul(
-                            columns(sums[u], i), lhsT=picked[i][:, halves[u]], rhs=ident[:], is_transpose=True,
-                            start=(d == 0 and i == 0 and u in opens), stop=(d == D - 1 and i == PAIR - 1 and u in closes),
+                            columns(region, i), lhsT=picked[i][:, halves[u]], rhs=ident[:], is_transpose=True,
+                            start=(d == 0 and i == 0 and opens), stop=(d == D - 1 and i == PAIR - 1 and closes),
                         )
-                all_turned.append(turned)
-                if d == 0:
-                    running.append(ring.tile([P, HALVES, PAIR, P], F32, name="running", tag="running0"))
-                    for u in range(HALVES):
-                        nc.scalar.activation(running[0][:, u, :, :], turned[:, u, :, :], ACT.Copy, scale=far_gates[:, u : u + 1])
-                after_list(d)
-                if split_last and d == 1:
-                    add_far(d)
 
-            return sums, add_far
+            def add_far(d, halves_of=range(HALVES), offset=None):
+                for u in halves_of:
+                    if offset is not None:
+                        running[d, u] = spot("held_running", [P, PAIR, P], F32, offset)
+                    elif d < D - 1:
+                        running[d, u] = ring.tile([P, PAIR, P], F32, name="running", tag="running")
+                    weight = far_gates[:, u, d : d + 1]
+                    if d == 0:
+                        nc.scalar.activation(running[0, u][:], turned[0][u], ACT.Copy, scale=weight)
+                    else:
+                        target = running[d, u][:] if d < D - 1 else place(2, u, rows)
+                        nc.vector.scalar_tensor_tensor(target, turned[d][u], weight, running[d - 1, u][:], MULT, ADD)
+
+            return far_list, near_list, add_far
 
         def quarter_columns(region, i):
             return region[:, :, 2 * QUAD * i : 2 * QUAD * (i + 1)]
@@ -243,27 +235,44 @@ def tile_picked_zmix_tanh_p_kernel(
 
         both = range(PAIR)
         lower_rows, upper_rows = slice(0, 2 * QUAD), slice(2 * QUAD, P)
-        h_upper = []
 
-        def make_upper(d):
-            if d == D - 1:
-                fetch_own(h_first, slice(0, QUAD), both, on_vector=True)
-                fetch_own(h_second, slice(QUAD, 2 * QUAD), both)
-            for a in range(PAIR if d == D - 1 else 0):
-                h_upper.append(make_h("h_upper%d" % a, upper_q[a], [(whole, "bc"[a])], on_vector=a == 1, pool=shared, offset=(14, 17)[a] * H_BYTES))
+        lower_sums = banks.tile([P, HALVES, PAIR, P], F32, name="lower_sums", tag="x")
+        far_list, near_list, add_lower = phase(
+            [h_first, h_second], quarter_columns, lower_rows, [(lower_sums[:, u, :, :], u == 0, u == HALVES - 1) for u in range(HALVES)]
+        )
+        far_list(0, "p", {1: 0})
+        near_list(0, {i: 11 * H_BYTES + 4 * V * i for i in both})
+        fetch_own(h_first, slice(0, QUAD), both)
+        fetch_own(h_second, slice(QUAD, 2 * QUAD), both)
+        h_upper = [make_h("h_upper%d" % a, upper_products[a]) for a in both]
+        for a in both:
+            fetch_own(h_upper[a], upper_rows, range(a, a + 1))
+        near_list(1, {i: 12 * H_BYTES + 4 * V * i for i in both})
+        near_list(2)
+        far_gates = keep.tile([P, HALVES, D], F32, name="far_gates")
+        for u, cols in enumerate(halves):
+            turned_gates = banks.tile([P, D, P], F32, name="turned_gates%d" % u, tag="rd"[u])
+            for d in range(D):
+                nc.tensor.transpose(turned_gates[:, d, :], wide_gates[d][:, cols], ident[:])
+            nc.scalar.copy(far_gates[:, u, :], turned_gates[:, :, 0])
+        far_list(1, "q")
+        far_list(2, "r")
+        add_lower(0)
+        nc.scalar.copy(place_near(lower_rows), lower_sums[:])
 
-        sums, add_lower = neighbours([h_first, h_second], quarter_columns, lower_rows, "x", "pqr", make_upper)
-        add_lower(1)
-        for u in range(HALVES):
-            nc.vector.tensor_copy(place(1, u, lower_rows), sums[u])
-
-        def finish_lower(d):
-            for a in range(PAIR if d == 0 else 0):
-                fetch_own(h_upper[a], upper_rows, range(a, a + 1))
-            if d == 1:
-                add_lower(D - 1)
-
-        sums, add_upper = neighbours(h_upper, slot_columns, upper_rows, "yb", "dpq", finish_lower)
+        near_sums = banks.tile([P, HALVES, PAIR, P], F32, name="near_sums", tag="y")
+        far_sums = [banks.tile([P, PAIR, P], F32, name="far_sums%d" % u, tag="db"[u]) for u in range(HALVES)]
+        unused, fused_list, unused = phase(
+            h_upper, slot_columns, upper_rows, [(near_sums[:, u, :, :], u == 0, u == HALVES - 1) for u in range(HALVES)]
+        )
+        fused_list(0, {i: 15 * H_BYTES + 4 * V * i for i in both})
+        fused_list(1)
+        fused_list(2)
+        far_parts = dict(lists=far, gates=wide_gates, sums=[(far_sums[u][:], True, True) for u in range(HALVES)])
+        fused_list(0, **far_parts)
+        nc.scalar.copy(place_near(upper_rows), near_sums[:])
+        fused_list(1, {0: 25 * H_BYTES}, **far_parts)
+        fused_list(2, by_halves=True, **far_parts)
         w_words = [load_words(words, "w_words%d" % i, shared, 15 * H_BYTES + 4 * N * i) for i, words in enumerate((w2_words, w3_words, w4_words))]
         staged_rows = shared.tile([16, 3 * N], U8, name="staged_rows", align_bytes=64, offset=0)
         for i, scales in enumerate((w2_scales, w3_scales, w4_scales)):
@@ -274,20 +283,28 @@ def tile_picked_zmix_tanh_p_kernel(
             nc.sync.dma_start(all_planes[32 * q : 32 * q + 4, :].bitcast(I32), staged_rows[4 * q : 4 * q + 4, :].bitcast(I32))
         w_planes = [all_planes[:, N * i : N * (i + 1)] for i in range(3)]
 
-        z_bf = [shared.tile([P, V, PACK], BF16, name="z_bf%d" % z, align_bytes=64, offset=(1 + z) * H_BYTES) for z in range(3)]
-        for u, cols in enumerate(halves):
-            nc.scalar.copy(place(1, u, upper_rows), sums[u])
-            near_back = banks.tile([P, PAIR, P], F32, name="near_back%d" % u, tag="xc"[u])
-            turn_back(near_back[:], 1, u)
-            nc.scalar.copy(words_of(z_bf[1][:, cols, :]), near_back[:].rearrange("p a v -> p v a"))
-        add_upper(D - 1)
-        for u, cols in enumerate(halves):
-            far_back = banks.tile([P, PAIR, P], F32, name="far_back%d" % u, tag="ry"[u])
-            turn_back(far_back[:], 2, u)
-            nc.scalar.copy(words_of(z_bf[2][:, cols, :]), far_back[:].rearrange("p a v -> p v a"))
+        z_own = keep.tile([P, V, PACK], BF16, name="z_own", align_bytes=64)
+        z_near = keep.tile([P, V, PACK], BF16, name="z_near", align_bytes=64)
+        z_far = [keep.tile([P, P, PACK], BF16, name="z_far%d" % u, align_bytes=64) for u in range(HALVES)]
 
-        def flat(z, cols):
-            return z_bf[z][:, cols, :].rearrange("p v t -> p (v t)")
+        near_back = banks.tile([P, HALVES, PAIR, P], F32, name="near_back", tag="c")
+        for u in range(HALVES):
+            turn_back(near_back[:, u, :, :], 1, u)
+        nc.scalar.copy(words_of(z_near[:]).rearrange("p (u v) a -> p u v a", u=HALVES), near_back[:].rearrange("p u a v -> p u v a"))
+        nc.scalar.copy(z_own[:, halves[0], :], own[:, :, halves[0]].rearrange("p t v -> p v t"))
+        for u in range(HALVES):
+            add_lower(1, (u,), 25 * H_BYTES - 512 + 1024 * u)
+        add_lower(2)
+        nc.vector.tensor_copy(z_own[:, halves[1], :], own[:, :, halves[1]].rearrange("p t v -> p v t"))
+        for u in range(HALVES):
+            nc.scalar.copy(place(2, u, upper_rows), far_sums[u][:])
+        for u in range(HALVES):
+            far_back = banks.tile([P, PAIR, P], F32, name="far_back%d" % u, tag="yx"[u])
+            turn_back(far_back[:], 2, u)
+            nc.scalar.copy(words_of(z_far[u][:]), far_back[:].rearrange("p a v -> p v a"))
+
+        def flat(values):
+            return values[:].rearrange("p v t -> p (v t)")
 
         def last_pass(result, z, codes, plane, start, stop):
             nc.tensor.matmul_mx(
@@ -295,14 +312,13 @@ def tile_picked_zmix_tanh_p_kernel(
                 rhs=codes.bitcast(FP8X4), rhs_scale=plane, start=start, stop=stop,
             )
 
-        results = [banks.tile([P, P], F32, name="result%d" % u, tag="dp"[u]) for u in range(HALVES)]
-        for cols in halves:
-            nc.vector.tensor_copy(z_bf[0][:, cols, :], own[:, :, cols].rearrange("p t v -> p v t"))
-        for z in range(2):
+        results = [banks.tile([P, P], F32, name="result%d" % u, tag="pq"[u]) for u in range(HALVES)]
+        for z, values in ((1, z_near), (0, z_own)):
+            codes, plane = quantize(flat(values), "z%d" % z)
             for u, cols in enumerate(halves):
-                last_pass(results[u], z, *quantize(flat(z, cols), "z%d_%d" % (z, u)), z == 0, False)
+                last_pass(results[u], z, codes[:, cols], plane[:, cols], z == 1, False)
         for u, cols in enumerate(halves):
-            last_pass(results[u], 2, *quantize(flat(2, cols), "z2_%d" % u), False, True)
+            last_pass(results[u], 2, *quantize(flat(z_far[u]), "z2_%d" % u), False, True)
             staged = keep.tile([P, P], F32, name="staged%d" % u)
             nc.scalar.activation(staged[:], results[u][:], ACT.Tanh)
             nc.sync.dma_start(out[:, cols], staged[:])

from contextlib import ExitStack

import concourse.mybir as mybir
from concourse.masks import make_identity

K, T, S, D, V, H, N = 512, 1024, 512, 3, 256, 512, 128
FLOPS = 2 * K * H * S + 3 * 2 * H * N * V

F32 = mybir.dt.float32
BF16 = mybir.dt.bfloat16
I32 = mybir.dt.int32
U32 = mybir.dt.uint32
U16 = mybir.dt.uint16
U8 = mybir.dt.uint8
FP8X4 = mybir.dt.float8_e4m3fn_x4
ACT = mybir.ActivationFunctionType
MULT = mybir.AluOpType.mult
ADD = mybir.AluOpType.add

P = 128
PACK = 4
PAIR = 2
HALVES = V // P
QUAD = P // 4
RING = 12
H_BYTES = 4 * S


def tile_picked_zmix_tanh_p_kernel(
    tc, x_words, x_scales, w1, w2_words, w2_scales, w3_words, w3_scales, w4_words, w4_scales,
    gate, gate2, offs, cen, pos1, pos2, pos3, far1, far2, far3, out,
):
    nc = tc.nc
    with ExitStack() as ctx:
        keep = ctx.enter_context(tc.tile_pool(name="keep", bufs=1))
        ring = ctx.enter_context(tc.tile_pool(name="ring", bufs=RING))
        shared = ctx.enter_context(tc.tile_pool(name="shared", bufs=1))
        banks = ctx.enter_context(tc.psum_pool(name="banks", bufs=1))

        def load_list(src, name):
            held = keep.tile(list(src.shape), U16, name=name)
            nc.sync.dma_start(held[:], src)
            return held

        def load_words(words, name, pool=keep, offset=None):
            held = pool.tile([P, words.shape[2]], I32, name=name, align_bytes=64, offset=offset)
            nc.sync.dma_start(held[:], words[0].rearrange("p n r -> p (n r)").bitcast(I32))
            return held

        def load_gates(weights, name):
            held = keep.tile([P, weights.shape[0], V], F32, name=name)
            nc.sync.dma_start(held[:], weights.rearrange("d p v -> p d v"))
            return [held[:, d, :] for d in range(weights.shape[0])]

        w1_rows = w1.rearrange("(p j) c -> p j c", j=PACK)

        offs_t = load_list(offs, "offs_t")
        x_plane = keep.tile([P, T], U8, name="x_plane", align_bytes=64)
        for q in range(4):
            rows = x_scales[0, 4 * q : 4 * q + 4, :].bitcast(I32)
            (nc.sync, nc.scalar)[q % 2].dma_start(x_plane[32 * q : 32 * q + 32, :].bitcast(I32), rows.unsqueeze(0).to_broadcast([8, 4, T // 4]))
        x_table = load_words(x_words, "x_table")
        first_raw = keep.tile([P, PACK, P], F32, name="first_raw")
        nc.sync.dma_start(first_raw[:], w1_rows[:, :, :P])
        second_raw = shared.tile([P, PACK, P], F32, name="second_raw", align_bytes=64, offset=14 * H_BYTES)
        nc.sync.dma_start(second_raw[:], w1_rows[:, :, P : 2 * P])
        upper_raw = shared.tile([P, PACK, 2 * P], F32, name="upper_raw", align_bytes=64, offset=11 * H_BYTES)
        nc.sync.dma_start(upper_raw[:], w1_rows[:, :, 2 * P :])
        far = [load_list(far1, "far0")]
        near_gates = load_gates(gate[:1], "first_gate")
        near = [load_list(pos1, "near0")]
        near.append(load_list(pos2, "near1"))
        near_gates = near_gates + load_gates(gate[1:], "later_gates")
        near.append(load_list(pos3, "near2"))
        cen_t = load_list(cen, "cen_t")
        far.append(load_list(far2, "far1"))
        far.append(load_list(far3, "far2"))
        wide_gates = load_gates(gate2, "wide_gates")

        ident = keep.tile([P, P], F32, name="ident")
        make_identity(nc, ident[:])

        def quantize(values, name, pool=keep, offset=None):
            width = values.shape[1] // PACK
            codes = pool.tile([P, width], U32, name=name + "_codes", align_bytes=64, offset=offset)
            plane = keep.tile([P, width], U8, name=name + "_plane", align_bytes=64)
            nc.vector.quantize_mx(out=codes[:].bitcast(FP8X4), scales=plane[:], in_=values)
            return codes[:], plane[:]

        halves = [slice(u * P, (u + 1) * P) for u in range(HALVES)]
        pieces = [slice(0, 256), slice(256, S)]

        def rounded_tile(name, pairs_of_slots, pool=keep, offset=None):
            shape = [P, pairs_of_slots, P // (PAIR * pairs_of_slots), PAIR, PACK]
            return pool.tile(shape, BF16, name=name, align_bytes=64, offset=offset)

        def walk_out(rounded):
            return rounded.rearrange("p a q s j -> p q j a s")

        def walk_in(raw):
            return raw.rearrange("p j (q a s) -> p q j a s", a=PAIR, s=PAIR)

        def flat_weights(rounded):
            return rounded[:].rearrange("p a q s j -> p (a q s j)")

        rounded_first = rounded_tile("rounded_first", PAIR)
        nc.scalar.copy(walk_out(rounded_first[:]), walk_in(first_raw[:]))

        x_scale = keep.tile([P, S], U8, name="x_scale", align_bytes=64)
        nc.vector.tensor_copy(x_scale[:], x_plane[:].indirect(offs_t[:]))
        first_q = quantize(flat_weights(rounded_first), "w1_first")
        x_codes = keep.tile([P, S], U32, name="x_codes", align_bytes=64)
        for cols in pieces:
            nc.vector.tensor_copy(x_codes[:, cols], x_table[:].bitcast(U32).indirect(offs_t[:, cols.start // 16 : cols.stop // 16]))

        def multiply(name, weights, parts):
            products = []
            for cols, bank in parts:
                acc = banks.tile([P, cols.stop - cols.start], F32, name="%s_%d" % (name, cols.start), tag=bank)
                nc.tensor.matmul_mx(
                    out=acc[:], lhsT=weights[0].bitcast(FP8X4), lhsT_scale=weights[1],
                    rhs=x_codes[:, cols].bitcast(FP8X4), rhs_scale=x_scale[:, cols],
                    start=True, stop=True,
                )
                products.append((cols, acc))
            return products

        def make_h(name, products, pool=keep, offset=None):
            h_n = pool.tile([P, S], F32, name=name, align_bytes=64, offset=offset)
            for cols, acc in products:
                nc.scalar.activation(h_n[:, cols], acc[:], ACT.Relu)
            return h_n

        whole = slice(0, S)
        rounded_second = rounded_tile("rounded_second", PAIR, shared, 13 * H_BYTES + H_BYTES // 4)
        nc.scalar.copy(walk_out(rounded_second[:]), walk_in(second_raw[:]))
        h_first = make_h("h_first", multiply("first", first_q, list(zip(pieces, "pq"))), shared, 14 * H_BYTES)
        h_second = make_h("h_second", multiply("second", quantize(flat_weights(rounded_second), "w1_second"), [(whole, "d")]))
        rounded_upper = [rounded_tile("rounded_upper%d" % a, 1, shared, 13 * H_BYTES + a * H_BYTES // 2) for a in range(PAIR)]
        for a in range(PAIR):
            nc.vector.tensor_copy(walk_out(rounded_upper[a][:]), walk_in(upper_raw[:])[:, :, :, a : a + 1, :])
        upper_q = [quantize(flat_weights(rounded_upper[a]), "w1_upper%d" % a) for a in range(PAIR)]
        upper_products = [multiply("upper%d" % a, upper_q[a], [(whole, "bc"[a])]) for a in range(PAIR)]


        own = keep.tile([P, PACK, V], BF16, name="own")

        def fetch_own(h_n, rows, slots, on_vector=False):
            values = ring.tile([P, V], BF16, name="own_values", tag="own")
            if on_vector:
                nc.vector.tensor_copy(values[:], h_n[:].indirect(cen_t[:]))
            else:
                nc.scalar.activation(values[:], h_n[:].indirect(cen_t[:]), ACT.Copy)
            count = PAIR * (rows.stop - rows.start)
            for i, a in enumerate(slots):
                nc.sync.dma_start(own[rows, PAIR * a : PAIR * (a + 1), :], values[count * i : count * (i + 1), :])

        near_pairs = keep.tile([P, HALVES, PAIR, P, PAIR], BF16, name="near_pairs", align_bytes=64)
        pairs = {
            1: [near_pairs[:, u, :, :, :] for u in range(HALVES)],
            2: [keep.tile([P, PAIR, P, PAIR], BF16, name="far_pairs%d" % u, align_bytes=64)[:] for u in range(HALVES)],
        }

        def place_near(rows):
            return near_pairs[:, :, :, rows, :].rearrange("v u a q s -> v u a (q s)")

        def place(z, u, rows):
            return pairs[z][u][:, :, rows, :].rearrange("v a q s -> v a (q s)")

        def spot(name, shape, dtype, offset):
            return shared.tile(shape, dtype, name=name, align_bytes=64, offset=offset)

        def phase(tiles, columns, rows, sums):
            turned, running = {}, {}

            def far_list(d, bank, spots={}):
                held = banks.tile([P, HALVES, PAIR, P], F32, name="turned", tag=bank)
                turned[d] = [held[:, u, :, :] for u in range(HALVES)]
                for i, h_n in enumerate(tiles):
                    if i in spots:
                        fetched = spot("held_fetched", [P, V], F32, spots[i])
                    else:
                        fetched = ring.tile([P, V], F32, name="fetched", tag="far", align_bytes=64)
                    nc.scalar.activation(fetched[:], h_n[:].indirect(far[d][:]), ACT.Copy)
                    for u, cols in enumerate(halves):
                        nc.tensor.transpose(columns(turned[d][u], i), fetched[:, cols], ident[:])

            def near_list(d, spots={}, by_halves=False, lists=near, gates=near_gates, sums=sums):
                picked = [
                    spot("held_picked", [P, V], F32, spots[i]) if i in spots else ring.tile([P, V], F32, name="picked", tag="near", align_bytes=64)
                    for i in range(PAIR)
                ]
                if by_halves:
                    steps = [(i, [u]) for u in range(HALVES) for i in range(PAIR)]
                else:
                    steps = [(i, range(HALVES)) for i in range(PAIR)]
                for i, us in steps:
                    cols = slice(halves[us[0]].start, halves[us[-1]].stop)
                    part = tiles[i][:].indirect(lists[d][:, cols.start // 16 : cols.stop // 16])
                    nc.vector.tensor_tensor(picked[i][:, cols], part, gates[d][:, cols], MULT)
                    for u in us:
                        region, opens, closes = sums[u]
                        nc.tensor.matmul(
                            columns(region, i), lhsT=picked[i][:, halves[u]], rhs=ident[:], is_transpose=True,
                            start=(d == 0 and i == 0 and opens), stop=(d == D - 1 and i == PAIR - 1 and closes),
                        )

            def add_far(d, halves_of=range(HALVES), offset=None):
                for u in halves_of:
                    if offset is not None:
                        running[d, u] = spot("held_running", [P, PAIR, P], F32, offset)
                    elif d < D - 1:
                        running[d, u] = ring.tile([P, PAIR, P], F32, name="running", tag="running")
                    weight = far_gates[:, u, d : d + 1]
                    if d == 0:
                        nc.scalar.activation(running[0, u][:], turned[0][u], ACT.Copy, scale=weight)
                    else:
                        target = running[d, u][:] if d < D - 1 else place(2, u, rows)
                        nc.vector.scalar_tensor_tensor(target, turned[d][u], weight, running[d - 1, u][:], MULT, ADD)

            return far_list, near_list, add_far

        def quarter_columns(region, i):
            return region[:, :, 2 * QUAD * i : 2 * QUAD * (i + 1)]

        def slot_columns(region, i):
            return region[:, i, :]

        def words_of(values):
            return values.rearrange("p v t -> p (v t)").bitcast(F32).rearrange("p (v a) -> p v a", a=PAIR)

        def turn_back(target, z, u):
            for a in range(PAIR):
                nc.tensor.transpose(target[:, a, :], pairs[z][u][:, a, :, :].rearrange("v p s -> v (p s)").bitcast(F32), ident[:])

        both = range(PAIR)
        lower_rows, upper_rows = slice(0, 2 * QUAD), slice(2 * QUAD, P)

        lower_sums = banks.tile([P, HALVES, PAIR, P], F32, name="lower_sums", tag="x")
        far_list, near_list, add_lower = phase(
            [h_first, h_second], quarter_columns, lower_rows, [(lower_sums[:, u, :, :], u == 0, u == HALVES - 1) for u in range(HALVES)]
        )
        far_list(0, "p", {1: 0})
        near_list(0, {i: 11 * H_BYTES + 4 * V * i for i in both})
        fetch_own(h_first, slice(0, QUAD), both)
        fetch_own(h_second, slice(QUAD, 2 * QUAD), both)
        h_upper = [make_h("h_upper%d" % a, upper_products[a]) for a in both]
        for a in both:
            fetch_own(h_upper[a], upper_rows, range(a, a + 1))
        near_list(1, {i: 12 * H_BYTES + 4 * V * i for i in both})
        near_list(2)
        far_gates = keep.tile([P, HALVES, D], F32, name="far_gates")
        for u, cols in enumerate(halves):
            turned_gates = banks.tile([P, D, P], F32, name="turned_gates%d" % u, tag="rd"[u])
            for d in range(D):
                nc.tensor.transpose(turned_gates[:, d, :], wide_gates[d][:, cols], ident[:])
            nc.scalar.copy(far_gates[:, u, :], turned_gates[:, :, 0])
        far_list(1, "q")
        far_list(2, "r")
        add_lower(0)
        nc.scalar.copy(place_near(lower_rows), lower_sums[:])

        near_sums = banks.tile([P, HALVES, PAIR, P], F32, name="near_sums", tag="y")
        far_sums = [banks.tile([P, PAIR, P], F32, name="far_sums%d" % u, tag="db"[u]) for u in range(HALVES)]
        unused, fused_list, unused = phase(
            h_upper, slot_columns, upper_rows, [(near_sums[:, u, :, :], u == 0, u == HALVES - 1) for u in range(HALVES)]
        )
        fused_list(0, {i: 15 * H_BYTES + 4 * V * i for i in both})
        fused_list(1)
        fused_list(2)
        far_parts = dict(lists=far, gates=wide_gates, sums=[(far_sums[u][:], True, True) for u in range(HALVES)])
        fused_list(0, **far_parts)
        nc.scalar.copy(place_near(upper_rows), near_sums[:])
        fused_list(1, {0: 25 * H_BYTES}, **far_parts)
        fused_list(2, by_halves=True, **far_parts)
        w_words = [load_words(words, "w_words%d" % i, shared, 15 * H_BYTES + 4 * N * i) for i, words in enumerate((w2_words, w3_words, w4_words))]
        staged_rows = shared.tile([16, 3 * N], U8, name="staged_rows", align_bytes=64, offset=0)
        for i, scales in enumerate((w2_scales, w3_scales, w4_scales)):
            nc.sync.dma_start(staged_rows[:, N * i : N * (i + 1)].bitcast(I32), scales[0].bitcast(I32))
        all_planes = keep.tile([P, 3 * N], U8, name="all_planes", align_bytes=64)
        nc.gpsimd.memset(all_planes[:].bitcast(I32), 0)
        for q in range(4):
            nc.sync.dma_start(all_planes[32 * q : 32 * q + 4, :].bitcast(I32), staged_rows[4 * q : 4 * q + 4, :].bitcast(I32))
        w_planes = [all_planes[:, N * i : N * (i + 1)] for i in range(3)]

        z_own = keep.tile([P, V, PACK], BF16, name="z_own", align_bytes=64)
        z_near = keep.tile([P, V, PACK], BF16, name="z_near", align_bytes=64)
        z_far = [keep.tile([P, P, PACK], BF16, name="z_far%d" % u, align_bytes=64) for u in range(HALVES)]

        near_back = banks.tile([P, HALVES, PAIR, P], F32, name="near_back", tag="c")
        for u in range(HALVES):
            turn_back(near_back[:, u, :, :], 1, u)
        nc.scalar.copy(words_of(z_near[:]).rearrange("p (u v) a -> p u v a", u=HALVES), near_back[:].rearrange("p u a v -> p u v a"))
        nc.scalar.copy(z_own[:, halves[0], :], own[:, :, halves[0]].rearrange("p t v -> p v t"))
        for u in range(HALVES):
            add_lower(1, (u,), 25 * H_BYTES - 512 + 1024 * u)
        add_lower(2)
        nc.vector.tensor_copy(z_own[:, halves[1], :], own[:, :, halves[1]].rearrange("p t v -> p v t"))
        for u in range(HALVES):
            nc.scalar.copy(place(2, u, upper_rows), far_sums[u][:])
        for u in range(HALVES):
            far_back = banks.tile([P, PAIR, P], F32, name="far_back%d" % u, tag="yx"[u])
            turn_back(far_back[:], 2, u)
            nc.scalar.copy(words_of(z_far[u][:]), far_back[:].rearrange("p a v -> p v a"))

        def flat(values):
            return values[:].rearrange("p v t -> p (v t)")

        def last_pass(result, z, codes, plane, start, stop):
            nc.tensor.matmul_mx(
                out=result[:], lhsT=w_words[z][:].bitcast(FP8X4), lhsT_scale=w_planes[z],
                rhs=codes.bitcast(FP8X4), rhs_scale=plane, start=start, stop=stop,
            )

        results = [banks.tile([P, P], F32, name="result%d" % u, tag="pq"[u]) for u in range(HALVES)]
        for z, values in ((1, z_near), (0, z_own)):
            codes, plane = quantize(flat(values), "z%d" % z)
            for u, cols in enumerate(halves):
                last_pass(results[u], z, codes[:, cols], plane[:, cols], z == 1, False)
        for u, cols in enumerate(halves):
            last_pass(results[u], 2, *quantize(flat(z_far[u]), "z2_%d" % u), False, True)
            staged = keep.tile([P, P], F32, name="staged%d" % u)
            nc.scalar.activation(staged[:], results[u][:], ACT.Tanh)
            nc.sync.dma_start(out[:, cols], staged[:])
